import numpy as np
import ml_dtypes


def mxq(x, axis, fmt="e4m3"):
    dtype, down = {"e4m3": (ml_dtypes.float8_e4m3fn, 7), "e5m2": (ml_dtypes.float8_e5m2, 14)}[fmt]
    v = np.moveaxis(np.asarray(x, np.float32).astype(ml_dtypes.bfloat16).astype(np.float64), axis, -1)
    blocks = v.reshape(v.shape[:-1] + (-1, 32))
    amax = np.abs(blocks).max(-1, keepdims=True)
    byte = np.maximum(np.where(amax > 0, np.frexp(amax)[1] - 1 + 127, 0) - down, 1)
    scale = np.exp2(byte - 127.0)
    codes = (blocks / scale).astype(np.float32).astype(dtype).astype(np.float64)
    return np.moveaxis((codes * scale).reshape(v.shape), -1, axis)


WIDE = False


def mx_kscale(k):
    if not WIDE:
        return np.ones(k)
    levels = np.array([10, -10, 5, -5, 0])
    if k % 512:
        return np.exp2(np.random.permutation(np.resize(levels, k // 32))).repeat(32)
    a = np.empty((k // 512, 16))
    for p in range(k // 512):
        a[p, :8] = np.random.permutation(np.resize(levels, 8))
        for g in range(8):
            far = levels[np.abs(levels - a[p, g]) >= 10]
            a[p, g + 8] = far[np.random.randint(len(far))]
    return np.exp2(a.ravel()).repeat(32)


def f64(x):
    return np.asarray(x).astype(np.float64)


def striped(idx):
    return np.tile(idx.reshape(-1, 16).T, (8, 1)).astype(np.uint16)


def unstriped(offs):
    return offs[:16].T.reshape(-1).astype(np.int64)


E2M1 = np.array([0.0, 0.5, 1.0, 1.5, 2.0, 3.0, 4.0, 6.0, -0.0, -0.5, -1.0, -1.5, -2.0, -3.0, -4.0, -6.0])


def pack_weight(w, fmt):
    k, n = w.shape
    w = f64(np.asarray(w, np.float32).astype(ml_dtypes.bfloat16)).reshape(k // 32, 32, n)
    amax = np.abs(w).max(1)
    if fmt == "e4m3":
        byte = np.frexp(amax)[1] - 1 + 127 - 7
    else:
        mant, ex = np.frexp(amax / 6.0)
        byte = np.where(mant > 0.5, ex, ex - 1) + 127
    byte = np.clip(np.where(amax > 0, byte, 1), 1, 254)
    scaled = (w * np.exp2(127.0 - byte)[:, None, :]).reshape(k, n).astype(np.float32)
    by_word = np.ascontiguousarray(scaled.reshape(k // 512, 128, 4, n).transpose(0, 1, 3, 2))
    if fmt == "e4m3":
        words = by_word.astype(ml_dtypes.float8_e4m3fn).view(np.uint8)
    else:
        c = by_word.astype(ml_dtypes.float4_e2m1fn).view(np.uint8) & 0xF
        words = (c[..., 0::2] | (c[..., 1::2] << 4)).reshape(k // 512, 128, 2 * n)
    return np.ascontiguousarray(words), np.ascontiguousarray(byte.astype(np.uint8).reshape(k // 512, 16, n))


def unpack_weight(words, scales, fmt):
    g, _, n = scales.shape
    words = np.ascontiguousarray(words).reshape(g, 128, n, -1)
    if fmt == "e4m3":
        vals = words.view(ml_dtypes.float8_e4m3fn).astype(np.float64)
    else:
        nib = np.empty((g, 128, n, 4), np.uint8)
        nib[..., 0::2] = words & 0xF
        nib[..., 1::2] = words >> 4
        vals = E2M1[nib]
    vals = vals * np.repeat(np.exp2(scales.astype(np.float64) - 127.0), 8, axis=1)[..., None]
    return vals.transpose(0, 1, 3, 2).reshape(g * 512, n)


def gelu(v):
    return 0.5 * v * (1.0 + np.tanh(np.sqrt(2.0 / np.pi) * (v + 0.044715 * v**3)))


def striped8(idx):
    return np.concatenate([v.reshape(-1, 16).T for v in idx]).astype(np.uint16)


def unstriped8(offs):
    return np.stack([offs[16 * g:16 * g + 16].T.reshape(-1) for g in range(8)]).astype(np.int64)


def runs(v, idx8):
    k = np.arange(v.shape[0])
    return v[k[:, None], idx8[k % 512 // 64]]


K, K2, H, N, T, S, T2 = 1024, 512, 1024, 512, 2048, 1024, 2048

def setup_inputs():
    n = np.random.standard_normal
    s, s2, u = mx_kscale(K)[:, None], mx_kscale(K2)[:, None], mx_kscale(H)[:, None]
    tab_words, tab_scales = pack_weight(n((K, T)) * s, "e4m3")
    tab2_words, tab2_scales = pack_weight(n((K2, T)) * s2, "e4m3")
    wb_words, wb_scales = pack_weight(n((K2, H)) / np.sqrt(K2) / s2, "e2m1")
    wq_words, wq_scales = pack_weight(1.3 * n((H, N)) / np.sqrt(H) / u, "e4m3")
    return {
        "tab_words": tab_words, "tab_scales": tab_scales,
        "offs": striped8(np.stack([np.random.permutation(T)[:S] for _ in range(8)])),
        "tab2_words": tab2_words, "tab2_scales": tab2_scales,
        "offs2": striped(np.random.permutation(T)[:S]),
        "offs3": striped(np.random.permutation(T2)[:S]),
        "wf": (n((K, H)) / np.sqrt(K) / s).astype(np.float32),
        "wb_words": wb_words, "wb_scales": wb_scales,
        "seam": n((H, S)).astype(np.float32),
        "gain": (np.exp(0.3 * n(H)) * u[:, 0]).astype(np.float32),
        "wq_words": wq_words, "wq_scales": wq_scales,
        "wgo": np.exp(0.3 * n((128, S))).astype(np.float32),
        "page1": n((N, T2)).astype(np.float32),
    }

def reference(tab_words, tab_scales, offs, tab2_words, tab2_scales, offs2, offs3, wf, wb_words, wb_scales,
              seam, gain, wq_words, wq_scales, wgo, page1):
    v = runs(unpack_weight(tab_words, tab_scales, "e4m3"), unstriped8(offs))
    v2 = unpack_weight(tab2_words, tab2_scales, "e4m3")[:, unstriped(offs2)]
    wb = unpack_weight(wb_words, wb_scales, "e2m1")
    wq = unpack_weight(wq_words, wq_scales, "e4m3")
    fabric = mxq(f64(wf), 0, "e4m3").T @ v
    pattern = wb.T @ v2
    z = np.tanh(f64(seam) * pattern + fabric) * f64(gain)[:, None]
    y = wq.T @ mxq(z, 0, "e4m3")
    out = f64(page1).copy()
    out[:, unstriped(offs3)] = np.tile(f64(wgo), (N // 128, 1)) * y
    return out

@@ -1,0 +1,239 @@
+from contextlib import ExitStack
+
+import concourse.mybir as mybir
+
+K, K2, H, N, T, S, T2 = 1024, 512, 1024, 512, 2048, 1024, 2048
+FLOPS = 2 * S * (K * H + K2 * H + H * N)
+
+F32 = mybir.dt.float32
+BF16 = mybir.dt.bfloat16
+I32 = mybir.dt.int32
+U32 = mybir.dt.uint32
+U16 = mybir.dt.uint16
+U8 = mybir.dt.uint8
+FP8X4 = mybir.dt.float8_e4m3fn_x4
+FP4X4 = mybir.dt.float4_e2m1fn_x4
+ACT = mybir.ActivationFunctionType
+ALU = mybir.AluOpType
+
+P = 128
+PACK = 4
+KP = P * PACK
+JC = 512
+LC = JC // 16
+
+
+def tile_list_quilt_patch_contrast_kernel(
+    tc, tab_words, tab_scales, offs, tab2_words, tab2_scales, offs2, offs3, wf, wb_words, wb_scales,
+    seam, gain, wq_words, wq_scales, wgo, page1, out,
+):
+    nc = tc.nc
+    na, nb, nh, ni = K // KP, H // KP, S // JC, N // P
+
+    with ExitStack() as ctx:
+        keep = ctx.enter_context(tc.tile_pool(name="keep", bufs=1))
+        stage = ctx.enter_context(tc.tile_pool(name="stage", bufs=2))
+        psum = ctx.enter_context(tc.psum_pool(name="psum", bufs=1))
+
+        def held(shape, dtype, name):
+            return keep.tile(shape, dtype, name=name, align_bytes=64)
+
+        list1 = held([P, S // 16], U16, "list1")
+        list2 = held([P, S // 16], U16, "list2")
+        list3 = held([P, S // 16], U16, "list3")
+        tab_sw = held([P, T], U8, "tab_sw")
+        tab2_sw = held([P, T], U8, "tab2_sw")
+        wb_s_raw = held([P, H], U8, "wb_s_raw")
+        wq_s = held([P, nb, N], U8, "wq_s")
+        nc.vector.memset(tab_sw[:].bitcast(I32), 0)
+        nc.vector.memset(tab2_sw[:].bitcast(I32), 0)
+        nc.vector.memset(wb_s_raw[:].bitcast(I32), 0)
+        nc.vector.memset(wq_s[:].rearrange("p b n -> p (b n)").bitcast(I32), 0)
+
+        def load_words(tile, src):
+            nc.sync.dma_start(tile[:].bitcast(I32), src.rearrange("p t i -> p (t i)").bitcast(I32))
+
+        tab2_w = held([P, T], U32, "tab2_w")
+        tab_w = [held([P, T], U32, "tab_w%d" % a) for a in range(na)]
+        wb_w_raw = held([P, H], U16, "wb_w_raw")
+        gain_t = held([P, nb, PACK], F32, "gain_t")
+        nc.sync.dma_start(list1[:], offs)
+        nc.sync.dma_start(wb_w_raw[:].bitcast(I32), wb_words[0].bitcast(I32))
+        nc.sync.dma_start(list2[:], offs2)
+        load_words(tab2_w, tab2_words[0])
+        for a in range(na):
+            load_words(tab_w[a], tab_words[a])
+        for a in range(na):
+            for e in range(2):
+                nc.scalar.dma_start(tab_sw[4 * a + e : P : 16, :].bitcast(I32), tab_scales[a, e:16:2, :].bitcast(I32))
+        for q in range(4):
+            nc.scalar.dma_start(
+                tab2_sw[32 * q : 32 * q + 4, :].bitcast(I32), tab2_scales[0, 4 * q : 4 * q + 4, :].bitcast(I32)
+            )
+        for q in range(4):
+            nc.gpsimd.dma_start(wb_s_raw[32 * q : 32 * q + 4, :].bitcast(I32), wb_scales[0, 4 * q : 4 * q + 4, :].bitcast(I32))
+        nc.gpsimd.dma_start(gain_t[:], gain.rearrange("(b p t) -> p b t", b=nb, t=PACK))
+        for q in range(4):
+            nc.gpsimd.dma_start(
+                wq_s[32 * q : 32 * q + 4, :, :].bitcast(I32),
+                wq_scales[:, 4 * q : 4 * q + 4, :].rearrange("b r n -> r b n").bitcast(I32),
+            )
+
+        wf_raw, seam_t, page = {}, {}, {}
+
+        def load_wf(b):
+            for a in range(na):
+                raw = keep.tile([P, PACK, KP], F32, name="wf_raw", bufs=4, align_bytes=64)
+                nc.sync.dma_start(
+                    raw[:], wf[KP * a : KP * (a + 1), KP * b : KP * (b + 1)].rearrange("(p j) c -> p j c", j=PACK)
+                )
+                wf_raw[a, b] = raw
+
+        def load_seam(b, h):
+            s = held([P, PACK, JC], F32, "seam%d%d" % (b, h))
+            nc.sync.dma_start(
+                s[:], seam[KP * b : KP * (b + 1), JC * h : JC * (h + 1)].rearrange("(p t) j -> p t j", t=PACK)
+            )
+            seam_t[b, h] = s
+
+        def load_page(i):
+            pg = held([P, T2], F32, "page%d" % i)
+            nc.sync.dma_start(pg[:], page1[P * i : P * (i + 1), :])
+            page[i] = pg
+
+        load_wf(0)
+        load_seam(0, 0)
+        load_wf(1)
+        load_seam(1, 0)
+        wq_w = held([P, nb, N], U32, "wq_w")
+        nc.sync.dma_start(wq_w[:].bitcast(I32), wq_words.rearrange("b p c i -> p b (c i)").bitcast(I32))
+        load_seam(0, 1)
+        nc.sync.dma_start(list3[:], offs3)
+        wgo_t = held([P, S], F32, "wgo_t")
+        nc.sync.dma_start(wgo_t[:], wgo)
+        for i in range(ni - 1):
+            load_page(i)
+        load_seam(1, 1)
+        load_page(ni - 1)
+
+        v_sg = held([P, S], U8, "v_sg")
+        nc.vector.tensor_copy(v_sg[:], tab_sw[:].indirect(list1[:]))
+        v_s = held([P, S], U8, "v_s")
+        nc.vector.tensor_copy(v_s[:].bitcast(I32), v_sg[:].bitcast(I32))
+        for a in range(na):
+            for e in range(2):
+                nc.scalar.dma_start(
+                    v_s[4 * a + 2 + e : P : 32, :].bitcast(I32), v_sg[16 + 4 * a + e : P : 32, :].bitcast(I32)
+                )
+        v2_s = held([P, S], U8, "v2_s")
+        nc.vector.tensor_copy(v2_s[:], tab2_sw[:].indirect(list2[:]))
+
+        wb_w = held([P, H], U16, "wb_w")
+        wb_s = held([P, H], U8, "wb_s")
+        nc.vector.tensor_copy(
+            wb_w[:].rearrange("p (b t m) -> p b m t", b=nb, t=PACK), wb_w_raw[:].rearrange("p (b m t) -> p b m t", b=nb, t=PACK)
+        )
+        nc.vector.tensor_copy(
+            wb_s[:].rearrange("p (b t m) -> p b m t", b=nb, t=PACK), wb_s_raw[:].rearrange("p (b m t) -> p b m t", b=nb, t=PACK)
+        )
+
+        v_w, v2_w, wf_w, wf_s, z_w, z_s = {}, {}, {}, {}, {}, {}
+
+        def gather_words(h):
+            cols = slice(LC * h, LC * (h + 1))
+            g = held([P, JC], U32, "v2_w%d" % h)
+            nc.vector.tensor_copy(g[:], tab2_w[:].indirect(list2[:, cols]))
+            v2_w[h] = g
+            for a in range(na):
+                g = held([P, JC], U32, "v_w%d%d" % (a, h))
+                nc.vector.tensor_copy(g[:], tab_w[a][:].indirect(list1[:, cols]))
+                v_w[a, h] = g
+
+        def quantize_wf(b):
+            for a in range(na):
+                grouped = stage.tile([P, KP * PACK], BF16, name="wf_grouped", align_bytes=64)
+                nc.scalar.copy(
+                    grouped[:].rearrange("p (t m j) -> p m j t", t=PACK, j=PACK),
+                    wf_raw[a, b][:].rearrange("p j (m t) -> p m j t", t=PACK),
+                )
+                wf_w[a, b] = held([P, KP], U32, "wf_w%d%d" % (a, b))
+                wf_s[a, b] = held([P, KP], U8, "wf_s%d%d" % (a, b))
+                nc.vector.quantize_mx(out=wf_w[a, b][:].bitcast(FP8X4), scales=wf_s[a, b][:], in_=grouped[:])
+
+        def first_stage(b, h):
+            jc = slice(JC * h, JC * (h + 1))
+            u = seam_t[b, h]
+            z_rows = stage.tile([P, PACK, JC], BF16, name="z_rows", align_bytes=64)
+
+            def pattern(t):
+                mc = slice(KP * b + P * t, KP * b + P * (t + 1))
+                acc = psum.tile([P, JC], F32, name="pattern", bufs=3)
+                nc.tensor.matmul_mx(
+                    out=acc[:], lhsT=wb_w[:, mc].bitcast(FP4X4), lhsT_scale=wb_s[:, mc],
+                    rhs=v2_w[h][:].bitcast(FP8X4), rhs_scale=v2_s[:, jc], start=True, stop=True,
+                )
+                nc.vector.tensor_tensor(u[:, t, :], acc[:], u[:, t, :], ALU.mult)
+
+            def fabric(t):
+                mc = slice(P * t, P * (t + 1))
+                acc = psum.tile([P, JC], F32, name="fabric", bufs=3)
+                for a in range(na):
+                    nc.tensor.matmul_mx(
+                        out=acc[:], lhsT=wf_w[a, b][:, mc].bitcast(FP8X4), lhsT_scale=wf_s[a, b][:, mc],
+                        rhs=v_w[a, h][:].bitcast(FP8X4), rhs_scale=v_s[4 * a : P, jc],
+                        start=(a == 0), stop=(a == na - 1),
+                    )
+                nc.vector.tensor_tensor(u[:, t, :], acc[:], u[:, t, :], ALU.add)
+                nc.scalar.activation(u[:, t, :], u[:, t, :], ACT.Tanh)
+                nc.scalar.activation(z_rows[:, t, :], u[:, t, :], ACT.Copy, scale=gain_t[:, b, t : t + 1])
+
+            pattern(0)
+            for t in range(PACK):
+                if t + 1 < PACK:
+                    pattern(t + 1)
+                fabric(t)
+            grouped = stage.tile([P, JC * PACK], BF16, name="z_grouped", align_bytes=64)
+            nc.scalar.copy(
+                grouped[:].rearrange("p (c i t) -> p c t i", i=4, t=PACK),
+                z_rows[:].rearrange("p t (c i) -> p c t i", i=4),
+            )
+            return grouped
+
+        def quantize_z(b, h, grouped):
+            z_w[b, h] = held([P, JC], U32, "z_w%d%d" % (b, h))
+            z_s[b, h] = held([P, JC], U8, "z_s%d%d" % (b, h))
+            nc.vector.quantize_mx(out=z_w[b, h][:].bitcast(FP8X4), scales=z_s[b, h][:], in_=grouped[:])
+
+        def second_stage(h, tiles):
+            for i in tiles:
+                mc = slice(P * i, P * (i + 1))
+                acc = psum.tile([P, JC], F32, name="contrast", bufs=2)
+                for b in range(nb):
+                    nc.tensor.matmul_mx(
+                        out=acc[:], lhsT=wq_w[:, b, mc].bitcast(FP8X4), lhsT_scale=wq_s[:, b, mc],
+                        rhs=z_w[b, h][:].bitcast(FP8X4), rhs_scale=z_s[b, h][:],
+                        start=(b == 0), stop=(b == nb - 1),
+                    )
+                y = stage.tile([P, JC], F32, name="y", bufs=6, align_bytes=64)
+                nc.scalar.copy(y[:], acc[:])
+                nc.vector.tensor_tensor(
+                    page[i][:].indirect(list3[:, LC * h : LC * (h + 1)]), y[:], wgo_t[:, JC * h : JC * (h + 1)], ALU.mult
+                )
+                if h == nh - 1:
+                    nc.sync.dma_start(out[P * i : P * (i + 1), :], page[i][:])
+
+        gather_words(0)
+        quantize_wf(0)
+        gather_words(1)
+        quantize_wf(1)
+        g00 = first_stage(0, 0)
+        g10 = first_stage(1, 0)
+        quantize_z(0, 0, g00)
+        quantize_z(1, 0, g10)
+        g01 = first_stage(0, 1)
+        quantize_z(0, 1, g01)
+        second_stage(0, range(ni - 1))
+        g11 = first_stage(1, 1)
+        quantize_z(1, 1, g11)
+        second_stage(0, [ni - 1])
+        second_stage(1, range(ni))

@@ -57,37 +57,14 @@ def tile_list_quilt_patch_contrast_kernel(
         tab_w = [held([P, T], U32, "tab_w%d" % a) for a in range(na)]
         wb_w_raw = held([P, H], U16, "wb_w_raw")
         gain_t = held([P, nb, PACK], F32, "gain_t")
-        nc.sync.dma_start(list1[:], offs)
-        nc.sync.dma_start(wb_w_raw[:].bitcast(I32), wb_words[0].bitcast(I32))
-        nc.sync.dma_start(list2[:], offs2)
-        load_words(tab2_w, tab2_words[0])
-        for a in range(na):
-            load_words(tab_w[a], tab_words[a])
-        for a in range(na):
-            for e in range(2):
-                nc.scalar.dma_start(tab_sw[4 * a + e : P : 16, :].bitcast(I32), tab_scales[a, e:16:2, :].bitcast(I32))
-        for q in range(4):
-            nc.scalar.dma_start(
-                tab2_sw[32 * q : 32 * q + 4, :].bitcast(I32), tab2_scales[0, 4 * q : 4 * q + 4, :].bitcast(I32)
-            )
-        for q in range(4):
-            nc.gpsimd.dma_start(wb_s_raw[32 * q : 32 * q + 4, :].bitcast(I32), wb_scales[0, 4 * q : 4 * q + 4, :].bitcast(I32))
-        nc.gpsimd.dma_start(gain_t[:], gain.rearrange("(b p t) -> p b t", b=nb, t=PACK))
-        for q in range(4):
-            nc.gpsimd.dma_start(
-                wq_s[32 * q : 32 * q + 4, :, :].bitcast(I32),
-                wq_scales[:, 4 * q : 4 * q + 4, :].rearrange("b r n -> r b n").bitcast(I32),
-            )
-
         wf_raw, seam_t, page = {}, {}, {}
 
-        def load_wf(b):
-            for a in range(na):
-                raw = keep.tile([P, PACK, KP], F32, name="wf_raw", bufs=4, align_bytes=64)
-                nc.sync.dma_start(
-                    raw[:], wf[KP * a : KP * (a + 1), KP * b : KP * (b + 1)].rearrange("(p j) c -> p j c", j=PACK)
-                )
-                wf_raw[a, b] = raw
+        def load_wf(a, b):
+            raw = held([P, PACK, KP], F32, "wf_raw%d%d" % (a, b))
+            nc.sync.dma_start(
+                raw[:], wf[KP * a : KP * (a + 1), KP * b : KP * (b + 1)].rearrange("(p j) c -> p j c", j=PACK)
+            )
+            wf_raw[a, b] = raw
 
         def load_seam(b, h):
             s = held([P, PACK, JC], F32, "seam%d%d" % (b, h))
@@ -101,20 +78,41 @@ def tile_list_quilt_patch_contrast_kernel(
             nc.sync.dma_start(pg[:], page1[P * i : P * (i + 1), :])
             page[i] = pg
 
-        load_wf(0)
+        for a in range(na):
+            for e in range(2):
+                nc.scalar.dma_start(tab_sw[4 * a + e : P : 16, :].bitcast(I32), tab_scales[a, e:16:2, :].bitcast(I32))
+        for q in range(4):
+            nc.gpsimd.dma_start(wb_s_raw[32 * q : 32 * q + 4, :].bitcast(I32), wb_scales[0, 4 * q : 4 * q + 4, :].bitcast(I32))
+        nc.gpsimd.dma_start(gain_t[:], gain.rearrange("(b p t) -> p b t", b=nb, t=PACK))
+        for q in range(4):
+            nc.gpsimd.dma_start(
+                wq_s[32 * q : 32 * q + 4, :, :].bitcast(I32),
+                wq_scales[:, 4 * q : 4 * q + 4, :].rearrange("b r n -> r b n").bitcast(I32),
+            )
+        nc.sync.dma_start(list1[:], offs)
+        nc.sync.dma_start(wb_w_raw[:].bitcast(I32), wb_words[0].bitcast(I32))
+        nc.sync.dma_start(list2[:], offs2)
+        load_words(tab2_w, tab2_words[0])
+        for a in range(na):
+            for q in (2 * a, 2 * a + 1):
+                nc.sync.dma_start(
+                    tab2_sw[32 * q : 32 * q + 4, :].bitcast(I32), tab2_scales[0, 4 * q : 4 * q + 4, :].bitcast(I32)
+                )
+            load_wf(a, 0)
+            load_words(tab_w[a], tab_words[a])
         load_seam(0, 0)
-        load_wf(1)
+        load_wf(0, 1)
+        load_wf(1, 1)
         load_seam(1, 0)
+        load_seam(0, 1)
+        load_seam(1, 1)
         wq_w = held([P, nb, N], U32, "wq_w")
         nc.sync.dma_start(wq_w[:].bitcast(I32), wq_words.rearrange("b p c i -> p b (c i)").bitcast(I32))
-        load_seam(0, 1)
         nc.sync.dma_start(list3[:], offs3)
         wgo_t = held([P, S], F32, "wgo_t")
         nc.sync.dma_start(wgo_t[:], wgo)
-        for i in range(ni - 1):
+        for i in range(ni):
             load_page(i)
-        load_seam(1, 1)
-        load_page(ni - 1)
 
         v_sg = held([P, S], U8, "v_sg")
         nc.vector.tensor_copy(v_sg[:], tab_sw[:].indirect(list1[:]))
@@ -149,91 +147,131 @@ def tile_list_quilt_patch_contrast_kernel(
                 nc.vector.tensor_copy(g[:], tab_w[a][:].indirect(list1[:, cols]))
                 v_w[a, h] = g
 
-        def quantize_wf(b):
+        wf_grouped = {}
+
+        def round_wf(a, b):
+            wf_grouped[a, b] = stage.tile([P, KP * PACK], BF16, name="wf_grouped", align_bytes=64)
+            nc.scalar.copy(
+                wf_grouped[a, b][:].rearrange("p (t m j) -> p m j t", t=PACK, j=PACK),
+                wf_raw[a, b][:].rearrange("p j (m t) -> p m j t", t=PACK),
+            )
+
+        def quantize_wf(a, b):
+            wf_w[a, b] = held([P, KP], U32, "wf_w%d%d" % (a, b))
+            wf_s[a, b] = held([P, KP], U8, "wf_s%d%d" % (a, b))
+            nc.vector.quantize_mx(out=wf_w[a, b][:].bitcast(FP8X4), scales=wf_s[a, b][:], in_=wf_grouped[a, b][:])
+
+        def pattern(b, h, t):
+            u = seam_t[b, h]
+            mc = slice(KP * b + P * t, KP * b + P * (t + 1))
+            acc = psum.tile([P, JC], F32, name="pattern", bufs=3)
+            nc.tensor.matmul_mx(
+                out=acc[:], lhsT=wb_w[:, mc].bitcast(FP4X4), lhsT_scale=wb_s[:, mc],
+                rhs=v2_w[h][:].bitcast(FP8X4), rhs_scale=v2_s[:, JC * h : JC * (h + 1)], start=True, stop=True,
+            )
+            nc.vector.tensor_tensor(u[:, t, :], acc[:], u[:, t, :], ALU.mult)
+
+        def fabric(b, h, t):
+            u = seam_t[b, h]
+            mc = slice(P * t, P * (t + 1))
+            acc = psum.tile([P, JC], F32, name="fabric", bufs=3)
             for a in range(na):
-                grouped = stage.tile([P, KP * PACK], BF16, name="wf_grouped", align_bytes=64)
-                nc.scalar.copy(
-                    grouped[:].rearrange("p (t m j) -> p m j t", t=PACK, j=PACK),
-                    wf_raw[a, b][:].rearrange("p j (m t) -> p m j t", t=PACK),
+                nc.tensor.matmul_mx(
+                    out=acc[:], lhsT=wf_w[a, b][:, mc].bitcast(FP8X4), lhsT_scale=wf_s[a, b][:, mc],
+                    rhs=v_w[a, h][:].bitcast(FP8X4), rhs_scale=v_s[4 * a : P, JC * h : JC * (h + 1)],
+                    start=(a == 0), stop=(a == na - 1),
                 )
-                wf_w[a, b] = held([P, KP], U32, "wf_w%d%d" % (a, b))
-                wf_s[a, b] = held([P, KP], U8, "wf_s%d%d" % (a, b))
-                nc.vector.quantize_mx(out=wf_w[a, b][:].bitcast(FP8X4), scales=wf_s[a, b][:], in_=grouped[:])
+            nc.vector.tensor_tensor(u[:, t, :], acc[:], u[:, t, :], ALU.add)
 
         def first_stage(b, h):
-            jc = slice(JC * h, JC * (h + 1))
-            u = seam_t[b, h]
-            z_rows = stage.tile([P, PACK, JC], BF16, name="z_rows", align_bytes=64)
-
-            def pattern(t):
-                mc = slice(KP * b + P * t, KP * b + P * (t + 1))
-                acc = psum.tile([P, JC], F32, name="pattern", bufs=3)
-                nc.tensor.matmul_mx(
-                    out=acc[:], lhsT=wb_w[:, mc].bitcast(FP4X4), lhsT_scale=wb_s[:, mc],
-                    rhs=v2_w[h][:].bitcast(FP8X4), rhs_scale=v2_s[:, jc], start=True, stop=True,
-                )
-                nc.vector.tensor_tensor(u[:, t, :], acc[:], u[:, t, :], ALU.mult)
-
-            def fabric(t):
-                mc = slice(P * t, P * (t + 1))
-                acc = psum.tile([P, JC], F32, name="fabric", bufs=3)
-                for a in range(na):
-                    nc.tensor.matmul_mx(
-                        out=acc[:], lhsT=wf_w[a, b][:, mc].bitcast(FP8X4), lhsT_scale=wf_s[a, b][:, mc],
-                        rhs=v_w[a, h][:].bitcast(FP8X4), rhs_scale=v_s[4 * a : P, jc],
-                        start=(a == 0), stop=(a == na - 1),
-                    )
-                nc.vector.tensor_tensor(u[:, t, :], acc[:], u[:, t, :], ALU.add)
-                nc.scalar.activation(u[:, t, :], u[:, t, :], ACT.Tanh)
-                nc.scalar.activation(z_rows[:, t, :], u[:, t, :], ACT.Copy, scale=gain_t[:, b, t : t + 1])
-
-            pattern(0)
+            pattern(b, h, 0)
             for t in range(PACK):
                 if t + 1 < PACK:
-                    pattern(t + 1)
-                fabric(t)
-            grouped = stage.tile([P, JC * PACK], BF16, name="z_grouped", align_bytes=64)
+                    pattern(b, h, t + 1)
+                fabric(b, h, t)
+
+        z_grouped = {}
+
+        def bend(b, h):
+            u = seam_t[b, h]
+            if (b, h) == (nb - 1, nh - 1):
+                z_rows = keep.tile([P, PACK, JC], BF16, name="z_rows_last", tag="last", align_bytes=64)
+            else:
+                z_rows = stage.tile([P, PACK, JC], BF16, name="z_rows", align_bytes=64)
+            for t in range(PACK):
+                nc.scalar.activation(u[:, t, :], u[:, t, :], ACT.Tanh)
+                if h == nh - 1:
+                    nc.scalar.activation(z_rows[:, t, :], u[:, t, :], ACT.Copy, scale=gain_t[:, b, t : t + 1])
+                else:
+                    nc.gpsimd.tensor_scalar(z_rows[:, t, :], u[:, t, :], gain_t[:, b, t : t + 1], 0.0, ALU.mult, ALU.add)
+            grouped = stage.tile([P, JC * PACK], BF16, name="z_grouped", bufs=3, align_bytes=64)
             nc.scalar.copy(
                 grouped[:].rearrange("p (c i t) -> p c t i", i=4, t=PACK),
                 z_rows[:].rearrange("p t (c i) -> p c t i", i=4),
             )
-            return grouped
+            z_grouped[b, h] = grouped
 
-        def quantize_z(b, h, grouped):
+        def quantize_z(b, h):
+            grouped = z_grouped[b, h]
             z_w[b, h] = held([P, JC], U32, "z_w%d%d" % (b, h))
             z_s[b, h] = held([P, JC], U8, "z_s%d%d" % (b, h))
             nc.vector.quantize_mx(out=z_w[b, h][:].bitcast(FP8X4), scales=z_s[b, h][:], in_=grouped[:])
 
-        def second_stage(h, tiles):
-            for i in tiles:
-                mc = slice(P * i, P * (i + 1))
-                acc = psum.tile([P, JC], F32, name="contrast", bufs=2)
-                for b in range(nb):
-                    nc.tensor.matmul_mx(
-                        out=acc[:], lhsT=wq_w[:, b, mc].bitcast(FP8X4), lhsT_scale=wq_s[:, b, mc],
-                        rhs=z_w[b, h][:].bitcast(FP8X4), rhs_scale=z_s[b, h][:],
-                        start=(b == 0), stop=(b == nb - 1),
-                    )
-                y = stage.tile([P, JC], F32, name="y", bufs=6, align_bytes=64)
-                nc.scalar.copy(y[:], acc[:])
-                nc.vector.tensor_tensor(
-                    page[i][:].indirect(list3[:, LC * h : LC * (h + 1)]), y[:], wgo_t[:, JC * h : JC * (h + 1)], ALU.mult
+        y = {}
+
+        def second_stage(h, i):
+            mc = slice(P * i, P * (i + 1))
+            acc = psum.tile([P, JC], F32, name="contrast", bufs=2)
+            for b in range(nb):
+                nc.tensor.matmul_mx(
+                    out=acc[:], lhsT=wq_w[:, b, mc].bitcast(FP8X4), lhsT_scale=wq_s[:, b, mc],
+                    rhs=z_w[b, h][:].bitcast(FP8X4), rhs_scale=z_s[b, h][:],
+                    start=(b == 0), stop=(b == nb - 1),
                 )
-                if h == nh - 1:
-                    nc.sync.dma_start(out[P * i : P * (i + 1), :], page[i][:])
+            if (h, i) == (0, ni - 1):
+                y[h, i] = keep.tile([P, JC], F32, name="y_last", tag="last", align_bytes=64)
+            else:
+                y[h, i] = stage.tile([P, JC], F32, name="y", bufs=4, align_bytes=64)
+            nc.scalar.copy(y[h, i][:], acc[:])
+
+        def place(h, i):
+            nc.vector.tensor_tensor(
+                page[i][:].indirect(list3[:, LC * h : LC * (h + 1)]), y[h, i][:], wgo_t[:, JC * h : JC * (h + 1)], ALU.mult
+            )
+            if h == nh - 1:
+                nc.sync.dma_start(out[P * i : P * (i + 1), :], page[i][:])
 
         gather_words(0)
-        quantize_wf(0)
+        for a in range(na):
+            round_wf(a, 0)
+            quantize_wf(a, 0)
         gather_words(1)
-        quantize_wf(1)
-        g00 = first_stage(0, 0)
-        g10 = first_stage(1, 0)
-        quantize_z(0, 0, g00)
-        quantize_z(1, 0, g10)
-        g01 = first_stage(0, 1)
-        quantize_z(0, 1, g01)
-        second_stage(0, range(ni - 1))
-        g11 = first_stage(1, 1)
-        quantize_z(1, 1, g11)
-        second_stage(0, [ni - 1])
-        second_stage(1, range(ni))
+        for a in range(na):
+            round_wf(a, 1)
+        first_stage(0, 0)
+        quantize_wf(0, 1)
+        for t in range(PACK):
+            pattern(1, 0, t)
+        quantize_wf(1, 1)
+        for t in range(PACK):
+            fabric(1, 0, t)
+        bend(0, 0)
+        bend(1, 0)
+        first_stage(0, 1)
+        quantize_z(0, 0)
+        quantize_z(1, 0)
+        first_stage(1, 1)
+        second_stage(0, 0)
+        second_stage(0, 1)
+        bend(0, 1)
+        second_stage(0, 2)
+        place(0, 0)
+        quantize_z(0, 1)
+        bend(1, 1)
+        quantize_z(1, 1)
+        second_stage(0, 3)
+        for i in range(1, ni):
+            place(0, i)
+        for i in range(ni):
+            second_stage(1, i)
+            place(1, i)

@@ -45,9 +45,9 @@ def tile_list_quilt_patch_contrast_kernel(
         tab2_sw = held([P, T], U8, "tab2_sw")
         wb_s_raw = held([P, H], U8, "wb_s_raw")
         wq_s = held([P, nb, N], U8, "wq_s")
-        nc.vector.memset(tab_sw[:].bitcast(I32), 0)
+        nc.gpsimd.memset(tab_sw[:].bitcast(I32), 0)
+        nc.gpsimd.memset(wb_s_raw[:].bitcast(I32), 0)
         nc.vector.memset(tab2_sw[:].bitcast(I32), 0)
-        nc.vector.memset(wb_s_raw[:].bitcast(I32), 0)
         nc.vector.memset(wq_s[:].rearrange("p b n -> p (b n)").bitcast(I32), 0)
 
         def load_words(tile, src):
@@ -66,12 +66,18 @@ def tile_list_quilt_patch_contrast_kernel(
             )
             wf_raw[a, b] = raw
 
-        def load_seam(b, h):
+        def load_seam(b, h, pieces=1):
             s = held([P, PACK, JC], F32, "seam%d%d" % (b, h))
-            nc.sync.dma_start(
-                s[:], seam[KP * b : KP * (b + 1), JC * h : JC * (h + 1)].rearrange("(p t) j -> p t j", t=PACK)
-            )
+            rows = seam[KP * b : KP * (b + 1), JC * h : JC * (h + 1)].rearrange("(p t) j -> p t j", t=PACK)
+            for t0 in range(0, PACK, PACK // pieces):
+                nc.sync.dma_start(s[:, t0 : t0 + PACK // pieces, :], rows[:, t0 : t0 + PACK // pieces, :])
             seam_t[b, h] = s
+
+        def load_tab2_scales(*quads):
+            for q in quads:
+                nc.sync.dma_start(
+                    tab2_sw[32 * q : 32 * q + 4, :].bitcast(I32), tab2_scales[0, 4 * q : 4 * q + 4, :].bitcast(I32)
+                )
 
         def load_page(i):
             pg = held([P, T2], F32, "page%d" % i)
@@ -81,33 +87,33 @@ def tile_list_quilt_patch_contrast_kernel(
         for a in range(na):
             for e in range(2):
                 nc.scalar.dma_start(tab_sw[4 * a + e : P : 16, :].bitcast(I32), tab_scales[a, e:16:2, :].bitcast(I32))
-        for q in range(4):
-            nc.gpsimd.dma_start(wb_s_raw[32 * q : 32 * q + 4, :].bitcast(I32), wb_scales[0, 4 * q : 4 * q + 4, :].bitcast(I32))
-        nc.gpsimd.dma_start(gain_t[:], gain.rearrange("(b p t) -> p b t", b=nb, t=PACK))
-        for q in range(4):
-            nc.gpsimd.dma_start(
-                wq_s[32 * q : 32 * q + 4, :, :].bitcast(I32),
-                wq_scales[:, 4 * q : 4 * q + 4, :].rearrange("b r n -> r b n").bitcast(I32),
-            )
         nc.sync.dma_start(list1[:], offs)
         nc.sync.dma_start(wb_w_raw[:].bitcast(I32), wb_words[0].bitcast(I32))
         nc.sync.dma_start(list2[:], offs2)
         load_words(tab2_w, tab2_words[0])
+        load_tab2_scales(0, 1, 2, 3)
+        load_wf(0, 0)
         for a in range(na):
+            load_words(tab_w[a], tab_words[a])
             for q in (2 * a, 2 * a + 1):
                 nc.sync.dma_start(
-                    tab2_sw[32 * q : 32 * q + 4, :].bitcast(I32), tab2_scales[0, 4 * q : 4 * q + 4, :].bitcast(I32)
+                    wb_s_raw[32 * q : 32 * q + 4, :].bitcast(I32), wb_scales[0, 4 * q : 4 * q + 4, :].bitcast(I32)
                 )
-            load_wf(a, 0)
-            load_words(tab_w[a], tab_words[a])
-        load_seam(0, 0)
+        nc.sync.dma_start(gain_t[:], gain.rearrange("(b p t) -> p b t", b=nb, t=PACK))
+        load_wf(1, 0)
         load_wf(0, 1)
+        load_seam(0, 0, pieces=2)
         load_wf(1, 1)
-        load_seam(1, 0)
+        load_seam(1, 0, pieces=2)
         load_seam(0, 1)
         load_seam(1, 1)
         wq_w = held([P, nb, N], U32, "wq_w")
         nc.sync.dma_start(wq_w[:].bitcast(I32), wq_words.rearrange("b p c i -> p b (c i)").bitcast(I32))
+        for q in range(4):
+            nc.sync.dma_start(
+                wq_s[32 * q : 32 * q + 4, :, :].bitcast(I32),
+                wq_scales[:, 4 * q : 4 * q + 4, :].rearrange("b r n -> r b n").bitcast(I32),
+            )
         nc.sync.dma_start(list3[:], offs3)
         wgo_t = held([P, S], F32, "wgo_t")
         nc.sync.dma_start(wgo_t[:], wgo)
@@ -130,9 +136,6 @@ def tile_list_quilt_patch_contrast_kernel(
         wb_s = held([P, H], U8, "wb_s")
         nc.vector.tensor_copy(
             wb_w[:].rearrange("p (b t m) -> p b m t", b=nb, t=PACK), wb_w_raw[:].rearrange("p (b m t) -> p b m t", b=nb, t=PACK)
-        )
-        nc.vector.tensor_copy(
-            wb_s[:].rearrange("p (b t m) -> p b m t", b=nb, t=PACK), wb_s_raw[:].rearrange("p (b m t) -> p b m t", b=nb, t=PACK)
         )
 
         v_w, v2_w, wf_w, wf_s, z_w, z_s = {}, {}, {}, {}, {}, {}
@@ -190,58 +193,67 @@ def tile_list_quilt_patch_contrast_kernel(
                     pattern(b, h, t + 1)
                 fabric(b, h, t)
 
-        z_grouped = {}
+        z_grouped, y = {}, {}
+        for h in range(nh):
+            for b in range(nb):
+                z_w[b, h] = held([P, JC], U32, "z_w%d%d" % (b, h))
+                z_s[b, h] = held([P, JC], U8, "z_s%d%d" % (b, h))
 
-        def bend(b, h):
-            u = seam_t[b, h]
-            if (b, h) == (nb - 1, nh - 1):
-                z_rows = keep.tile([P, PACK, JC], BF16, name="z_rows_last", tag="last", align_bytes=64)
+        def bend(b, j0, w, tag=None):
+            u, jc = seam_t[b, j0 // JC], slice(j0 % JC, j0 % JC + w)
+            if tag is None:
+                z_rows = stage.tile([P, PACK, w], BF16, name="z_rows", align_bytes=64)
             else:
-                z_rows = stage.tile([P, PACK, JC], BF16, name="z_rows", align_bytes=64)
+                z_rows = keep.tile([P, PACK, w], BF16, name="z_rows_" + tag, tag=tag, align_bytes=64)
+            if j0 >= JC:
+                nc.scalar.activation(u[:, :, jc], u[:, :, jc], ACT.Tanh)
             for t in range(PACK):
-                nc.scalar.activation(u[:, t, :], u[:, t, :], ACT.Tanh)
-                if h == nh - 1:
-                    nc.scalar.activation(z_rows[:, t, :], u[:, t, :], ACT.Copy, scale=gain_t[:, b, t : t + 1])
+                if j0 >= JC:
+                    nc.scalar.activation(z_rows[:, t, :], u[:, t, jc], ACT.Copy, scale=gain_t[:, b, t : t + 1])
                 else:
-                    nc.gpsimd.tensor_scalar(z_rows[:, t, :], u[:, t, :], gain_t[:, b, t : t + 1], 0.0, ALU.mult, ALU.add)
-            grouped = stage.tile([P, JC * PACK], BF16, name="z_grouped", bufs=3, align_bytes=64)
+                    nc.scalar.activation(u[:, t, jc], u[:, t, jc], ACT.Tanh)
+                    nc.gpsimd.tensor_scalar(z_rows[:, t, :], u[:, t, jc], gain_t[:, b, t : t + 1], 0.0, ALU.mult, ALU.add)
+            z_grouped[b, j0] = stage.tile([P, w * PACK], BF16, name="z_grouped", bufs=3, align_bytes=64)
             nc.scalar.copy(
-                grouped[:].rearrange("p (c i t) -> p c t i", i=4, t=PACK),
+                z_grouped[b, j0][:].rearrange("p (c i t) -> p c t i", i=4, t=PACK),
                 z_rows[:].rearrange("p t (c i) -> p c t i", i=4),
             )
-            z_grouped[b, h] = grouped
 
-        def quantize_z(b, h):
-            grouped = z_grouped[b, h]
-            z_w[b, h] = held([P, JC], U32, "z_w%d%d" % (b, h))
-            z_s[b, h] = held([P, JC], U8, "z_s%d%d" % (b, h))
-            nc.vector.quantize_mx(out=z_w[b, h][:].bitcast(FP8X4), scales=z_s[b, h][:], in_=grouped[:])
+        def quantize_z(b, j0, w):
+            h, jc = j0 // JC, slice(j0 % JC, j0 % JC + w)
+            nc.vector.quantize_mx(out=z_w[b, h][:, jc].bitcast(FP8X4), scales=z_s[b, h][:, jc], in_=z_grouped[b, j0][:])
 
-        y = {}
-
-        def second_stage(h, i):
+        def second_stage(i, j0, w, tag=None):
+            h, jc = j0 // JC, slice(j0 % JC, j0 % JC + w)
             mc = slice(P * i, P * (i + 1))
-            acc = psum.tile([P, JC], F32, name="contrast", bufs=2)
+            if j0 < JC:
+                acc = psum.tile([P, w], F32, name="contrast", bufs=2)
+            else:
+                acc = psum.tile([P, w], F32, name="contrast_late", tag="pattern" if i % 2 == 0 else "fabric", bufs=3)
             for b in range(nb):
                 nc.tensor.matmul_mx(
                     out=acc[:], lhsT=wq_w[:, b, mc].bitcast(FP8X4), lhsT_scale=wq_s[:, b, mc],
-                    rhs=z_w[b, h][:].bitcast(FP8X4), rhs_scale=z_s[b, h][:],
+                    rhs=z_w[b, h][:, jc].bitcast(FP8X4), rhs_scale=z_s[b, h][:, jc],
                     start=(b == 0), stop=(b == nb - 1),
                 )
-            if (h, i) == (0, ni - 1):
-                y[h, i] = keep.tile([P, JC], F32, name="y_last", tag="last", align_bytes=64)
+            if tag is None:
+                y[i, j0] = stage.tile([P, w], F32, name="y", bufs=4, align_bytes=64)
             else:
-                y[h, i] = stage.tile([P, JC], F32, name="y", bufs=4, align_bytes=64)
-            nc.scalar.copy(y[h, i][:], acc[:])
+                y[i, j0] = keep.tile([P, w], F32, name="y_" + tag, tag=tag, align_bytes=64)
+            nc.scalar.copy(y[i, j0][:], acc[:])
 
-        def place(h, i):
+        def place(i, j0, w):
             nc.vector.tensor_tensor(
-                page[i][:].indirect(list3[:, LC * h : LC * (h + 1)]), y[h, i][:], wgo_t[:, JC * h : JC * (h + 1)], ALU.mult
+                page[i][:].indirect(list3[:, j0 // 16 : (j0 + w) // 16]), y[i, j0][:], wgo_t[:, j0 : j0 + w], ALU.mult
             )
-            if h == nh - 1:
+            if j0 + w == S:
                 nc.sync.dma_start(out[P * i : P * (i + 1), :], page[i][:])
 
+        Q3, Q4, QW = JC, JC + JC // 2, JC // 2
         gather_words(0)
+        nc.vector.tensor_copy(
+            wb_s[:].rearrange("p (b t m) -> p b m t", b=nb, t=PACK), wb_s_raw[:].rearrange("p (b m t) -> p b m t", b=nb, t=PACK)
+        )
         for a in range(na):
             round_wf(a, 0)
             quantize_wf(a, 0)
@@ -250,28 +262,47 @@ def tile_list_quilt_patch_contrast_kernel(
             round_wf(a, 1)
         first_stage(0, 0)
         quantize_wf(0, 1)
-        for t in range(PACK):
-            pattern(1, 0, t)
+        pattern(1, 0, 0)
+        pattern(1, 0, 1)
         quantize_wf(1, 1)
+        pattern(1, 0, 2)
+        pattern(1, 0, 3)
         for t in range(PACK):
             fabric(1, 0, t)
-        bend(0, 0)
-        bend(1, 0)
+        bend(0, 0, JC)
+        bend(1, 0, JC)
         first_stage(0, 1)
-        quantize_z(0, 0)
-        quantize_z(1, 0)
-        first_stage(1, 1)
-        second_stage(0, 0)
-        second_stage(0, 1)
-        bend(0, 1)
-        second_stage(0, 2)
-        place(0, 0)
-        quantize_z(0, 1)
-        bend(1, 1)
-        quantize_z(1, 1)
-        second_stage(0, 3)
-        for i in range(1, ni):
-            place(0, i)
-        for i in range(ni):
-            second_stage(1, i)
-            place(1, i)
+        quantize_z(0, 0, JC)
+        pattern(1, 1, 0)
+        pattern(1, 1, 1)
+        fabric(1, 1, 0)
+        pattern(1, 1, 2)
+        quantize_z(1, 0, JC)
+        fabric(1, 1, 1)
+        pattern(1, 1, 3)
+        fabric(1, 1, 2)
+        fabric(1, 1, 3)
+        for i in range(ni - 1):
+            second_stage(i, 0, JC)
+        bend(0, Q3, QW)
+        bend(1, Q3, QW, "third")
+        for i in range(ni - 1):
+            place(i, 0, JC)
+        for b in range(nb):
+            quantize_z(b, Q3, QW)
+        second_stage(ni - 1, 0, JC, "third")
+        bend(0, Q4, QW)
+        bend(1, Q4, QW, "fourth")
+        place(ni - 1, 0, JC)
+        for b in range(nb):
+            quantize_z(b, Q4, QW)
+        second_stage(0, Q3, QW, "fourth")
+        second_stage(1, Q3, QW)
+        place(0, Q3, QW)
+        place(1, Q3, QW)
+        for i in range(2):
+            second_stage(i, Q4, QW)
+            place(i, Q4, QW)
+        for i in range(2, ni):
+            second_stage(i, JC, JC)
+            place(i, JC, JC)

@@ -79,6 +79,12 @@ def tile_list_quilt_patch_contrast_kernel(
                     tab2_sw[32 * q : 32 * q + 4, :].bitcast(I32), tab2_scales[0, 4 * q : 4 * q + 4, :].bitcast(I32)
                 )
 
+        def load_wb_scales(*quads):
+            for q in quads:
+                nc.sync.dma_start(
+                    wb_s_raw[32 * q : 32 * q + 4, :].bitcast(I32), wb_scales[0, 4 * q : 4 * q + 4, :].bitcast(I32)
+                )
+
         def load_page(i):
             pg = held([P, T2], F32, "page%d" % i)
             nc.sync.dma_start(pg[:], page1[P * i : P * (i + 1), :])
@@ -93,14 +99,12 @@ def tile_list_quilt_patch_contrast_kernel(
         load_words(tab2_w, tab2_words[0])
         load_tab2_scales(0, 1, 2, 3)
         load_wf(0, 0)
-        for a in range(na):
-            load_words(tab_w[a], tab_words[a])
-            for q in (2 * a, 2 * a + 1):
-                nc.sync.dma_start(
-                    wb_s_raw[32 * q : 32 * q + 4, :].bitcast(I32), wb_scales[0, 4 * q : 4 * q + 4, :].bitcast(I32)
-                )
-        nc.sync.dma_start(gain_t[:], gain.rearrange("(b p t) -> p b t", b=nb, t=PACK))
+        load_words(tab_w[0], tab_words[0])
+        load_wb_scales(0, 1)
         load_wf(1, 0)
+        load_wb_scales(2, 3)
+        nc.sync.dma_start(gain_t[:], gain.rearrange("(b p t) -> p b t", b=nb, t=PACK))
+        load_words(tab_w[1], tab_words[1])
         load_wf(0, 1)
         load_seam(0, 0, pieces=2)
         load_wf(1, 1)
@@ -199,25 +203,35 @@ def tile_list_quilt_patch_contrast_kernel(
                 z_w[b, h] = held([P, JC], U32, "z_w%d%d" % (b, h))
                 z_s[b, h] = held([P, JC], U8, "z_s%d%d" % (b, h))
 
-        def bend(b, j0, w, tag=None):
+        def bend(b, j0, w, on_gpsimd=0, tag=None):
             u, jc = seam_t[b, j0 // JC], slice(j0 % JC, j0 % JC + w)
             if tag is None:
-                z_rows = stage.tile([P, PACK, w], BF16, name="z_rows", align_bytes=64)
+                rows = stage.tile([P, PACK, w], BF16, name="z_rows", align_bytes=64)
             else:
-                z_rows = keep.tile([P, PACK, w], BF16, name="z_rows_" + tag, tag=tag, align_bytes=64)
-            if j0 >= JC:
-                nc.scalar.activation(u[:, :, jc], u[:, :, jc], ACT.Tanh)
+                rows = keep.tile([P, PACK, w], BF16, name="z_rows_" + tag, tag=tag, align_bytes=64)
             for t in range(PACK):
-                if j0 >= JC:
-                    nc.scalar.activation(z_rows[:, t, :], u[:, t, jc], ACT.Copy, scale=gain_t[:, b, t : t + 1])
+                nc.scalar.activation(u[:, t, jc], u[:, t, jc], ACT.Tanh)
+                if t < on_gpsimd:
+                    nc.gpsimd.tensor_scalar(rows[:, t, :], u[:, t, jc], gain_t[:, b, t : t + 1], 0.0, ALU.mult, ALU.add)
                 else:
-                    nc.scalar.activation(u[:, t, jc], u[:, t, jc], ACT.Tanh)
-                    nc.gpsimd.tensor_scalar(z_rows[:, t, :], u[:, t, jc], gain_t[:, b, t : t + 1], 0.0, ALU.mult, ALU.add)
-            z_grouped[b, j0] = stage.tile([P, w * PACK], BF16, name="z_grouped", bufs=3, align_bytes=64)
+                    nc.scalar.activation(rows[:, t, :], u[:, t, jc], ACT.Copy, scale=gain_t[:, b, t : t + 1])
+            return rows
+
+        def weave(b, j0, rows):
+            z_grouped[b, j0] = stage.tile([P, rows.shape[2] * PACK], BF16, name="z_grouped", bufs=3, align_bytes=64)
             nc.scalar.copy(
                 z_grouped[b, j0][:].rearrange("p (c i t) -> p c t i", i=4, t=PACK),
-                z_rows[:].rearrange("p t (c i) -> p c t i", i=4),
+                rows.rearrange("p t (c i) -> p c t i", i=4),
             )
+
+        def weave_on_gpsimd(b, j0, rows):
+            w = rows.shape[2]
+            z_grouped[b, j0] = stage.tile([P, w * PACK], BF16, name="z_grouped", bufs=3, align_bytes=64)
+            for c0 in range(0, w, w // 2):
+                nc.gpsimd.tensor_scalar(
+                    z_grouped[b, j0][:, PACK * c0 : PACK * (c0 + w // 2)].rearrange("p (j t) -> p j t", t=PACK),
+                    rows[:, :, c0 : c0 + w // 2].rearrange("p t j -> p j t"), 1.0, 0.0, ALU.mult, ALU.add,
+                )
 
         def quantize_z(b, j0, w):
             h, jc = j0 // JC, slice(j0 % JC, j0 % JC + w)
@@ -269,30 +283,33 @@ def tile_list_quilt_patch_contrast_kernel(
         pattern(1, 0, 3)
         for t in range(PACK):
             fabric(1, 0, t)
-        bend(0, 0, JC)
-        bend(1, 0, JC)
+        weave_on_gpsimd(0, 0, bend(0, 0, JC, on_gpsimd=3)[:])
+        weave(1, 0, bend(1, 0, JC, on_gpsimd=2)[:])
         first_stage(0, 1)
         quantize_z(0, 0, JC)
         pattern(1, 1, 0)
         pattern(1, 1, 1)
         fabric(1, 1, 0)
-        pattern(1, 1, 2)
         quantize_z(1, 0, JC)
+        pattern(1, 1, 2)
         fabric(1, 1, 1)
         pattern(1, 1, 3)
         fabric(1, 1, 2)
         fabric(1, 1, 3)
         for i in range(ni - 1):
             second_stage(i, 0, JC)
-        bend(0, Q3, QW)
-        bend(1, Q3, QW, "third")
+        low_rows = bend(0, JC, JC)
+        third_rows = bend(1, Q3, QW, tag="third")
+        weave(0, Q3, low_rows[:, :, :QW])
+        weave(1, Q3, third_rows[:])
         for i in range(ni - 1):
             place(i, 0, JC)
         for b in range(nb):
             quantize_z(b, Q3, QW)
         second_stage(ni - 1, 0, JC, "third")
-        bend(0, Q4, QW)
-        bend(1, Q4, QW, "fourth")
+        fourth_rows = bend(1, Q4, QW, tag="fourth")
+        weave(0, Q4, low_rows[:, :, QW:])
+        weave(1, Q4, fourth_rows[:])
         place(ni - 1, 0, JC)
         for b in range(nb):
             quantize_z(b, Q4, QW)
@@ -300,7 +317,7 @@ def tile_list_quilt_patch_contrast_kernel(
         second_stage(1, Q3, QW)
         place(0, Q3, QW)
         place(1, Q3, QW)
-        for i in range(2):
+        for i in (1, 0):
             second_stage(i, Q4, QW)
             place(i, Q4, QW)
         for i in range(2, ni):

@@ -18,9 +18,17 @@ ALU = mybir.AluOpType
 
 P = 128
 PACK = 4
-KP = P * PACK
-JC = 512
-LC = JC // 16
+PASS = P * PACK
+QUAD = 32
+QUADS = P // QUAD
+LIVE = 4
+BLOCKS = QUADS * LIVE
+GROUP = 16
+HALF = 512
+QUARTER = HALF // 2
+K_PASSES, R_PASSES, ROW_TILES = K // PASS, H // PASS, N // P
+
+GAINS_ON_GPSIMD = (3, 2)
 
 
 def tile_list_quilt_patch_contrast_kernel(
@@ -28,7 +36,6 @@ def tile_list_quilt_patch_contrast_kernel(
     seam, gain, wq_words, wq_scales, wgo, page1, out,
 ):
     nc = tc.nc
-    na, nb, nh, ni = K // KP, H // KP, S // JC, N // P
 
     with ExitStack() as ctx:
         keep = ctx.enter_context(tc.tile_pool(name="keep", bufs=1))
@@ -38,288 +45,289 @@ def tile_list_quilt_patch_contrast_kernel(
         def held(shape, dtype, name):
             return keep.tile(shape, dtype, name=name, align_bytes=64)
 
-        list1 = held([P, S // 16], U16, "list1")
-        list2 = held([P, S // 16], U16, "list2")
-        list3 = held([P, S // 16], U16, "list3")
-        tab_sw = held([P, T], U8, "tab_sw")
-        tab2_sw = held([P, T], U8, "tab2_sw")
-        wb_s_raw = held([P, H], U8, "wb_s_raw")
-        wq_s = held([P, nb, N], U8, "wq_s")
-        nc.gpsimd.memset(tab_sw[:].bitcast(I32), 0)
-        nc.gpsimd.memset(wb_s_raw[:].bitcast(I32), 0)
-        nc.vector.memset(tab2_sw[:].bitcast(I32), 0)
-        nc.vector.memset(wq_s[:].rearrange("p b n -> p (b n)").bitcast(I32), 0)
+        list1 = held([P, S // GROUP], U16, "list1")
+        list2 = held([P, S // GROUP], U16, "list2")
+        list3 = held([P, S // GROUP], U16, "list3")
+        tab_bytes = held([P, T], U8, "tab_bytes")
+        tab2_bytes = held([P, T], U8, "tab2_bytes")
+        wb_bytes = held([P, H], U8, "wb_bytes")
+        wq_planes = held([P, R_PASSES, N], U8, "wq_planes")
+        nc.gpsimd.memset(tab_bytes[:].bitcast(I32), 0)
+        nc.gpsimd.memset(wb_bytes[:].bitcast(I32), 0)
+        nc.vector.memset(tab2_bytes[:].bitcast(I32), 0)
+        nc.vector.memset(wq_planes[:].rearrange("p b n -> p (b n)").bitcast(I32), 0)
 
-        def load_words(tile, src):
-            nc.sync.dma_start(tile[:].bitcast(I32), src.rearrange("p t i -> p (t i)").bitcast(I32))
+        tab2_window = held([P, T], U32, "tab2_window")
+        tab_window = [held([P, T], U32, "tab_window%d" % a) for a in range(K_PASSES)]
+        wb_loaded = held([P, H], U16, "wb_loaded")
+        gain_sb = held([P, R_PASSES, PACK], F32, "gain_sb")
+        wf_loaded, pre, page = {}, {}, {}
 
-        tab2_w = held([P, T], U32, "tab2_w")
-        tab_w = [held([P, T], U32, "tab_w%d" % a) for a in range(na)]
-        wb_w_raw = held([P, H], U16, "wb_w_raw")
-        gain_t = held([P, nb, PACK], F32, "gain_t")
-        wf_raw, seam_t, page = {}, {}, {}
+        def load_tab(a):
+            nc.sync.dma_start(tab_window[a][:].bitcast(I32), tab_words[a].rearrange("p t i -> p (t i)").bitcast(I32))
+
+        def load_plane(tile, scales, quads):
+            for d in quads:
+                nc.sync.dma_start(
+                    tile[QUAD * d : QUAD * d + LIVE, :].bitcast(I32), scales[LIVE * d : LIVE * (d + 1), :].bitcast(I32)
+                )
 
         def load_wf(a, b):
-            raw = held([P, PACK, KP], F32, "wf_raw%d%d" % (a, b))
+            wf_loaded[a, b] = held([P, PACK, PASS], F32, "wf_loaded%d%d" % (a, b))
             nc.sync.dma_start(
-                raw[:], wf[KP * a : KP * (a + 1), KP * b : KP * (b + 1)].rearrange("(p j) c -> p j c", j=PACK)
+                wf_loaded[a, b][:],
+                wf[PASS * a : PASS * (a + 1), PASS * b : PASS * (b + 1)].rearrange("(p i) c -> p i c", i=PACK),
             )
-            wf_raw[a, b] = raw
 
-        def load_seam(b, h, pieces=1):
-            s = held([P, PACK, JC], F32, "seam%d%d" % (b, h))
-            rows = seam[KP * b : KP * (b + 1), JC * h : JC * (h + 1)].rearrange("(p t) j -> p t j", t=PACK)
+        def load_seam(b, h, pieces):
+            pre[b, h] = held([P, PACK, HALF], F32, "pre%d%d" % (b, h))
+            source = seam[PASS * b : PASS * (b + 1), HALF * h : HALF * (h + 1)].rearrange("(p t) j -> p t j", t=PACK)
             for t0 in range(0, PACK, PACK // pieces):
-                nc.sync.dma_start(s[:, t0 : t0 + PACK // pieces, :], rows[:, t0 : t0 + PACK // pieces, :])
-            seam_t[b, h] = s
+                nc.sync.dma_start(pre[b, h][:, t0 : t0 + PACK // pieces, :], source[:, t0 : t0 + PACK // pieces, :])
 
-        def load_tab2_scales(*quads):
-            for q in quads:
-                nc.sync.dma_start(
-                    tab2_sw[32 * q : 32 * q + 4, :].bitcast(I32), tab2_scales[0, 4 * q : 4 * q + 4, :].bitcast(I32)
-                )
-
-        def load_wb_scales(*quads):
-            for q in quads:
-                nc.sync.dma_start(
-                    wb_s_raw[32 * q : 32 * q + 4, :].bitcast(I32), wb_scales[0, 4 * q : 4 * q + 4, :].bitcast(I32)
-                )
-
-        def load_page(i):
-            pg = held([P, T2], F32, "page%d" % i)
-            nc.sync.dma_start(pg[:], page1[P * i : P * (i + 1), :])
-            page[i] = pg
-
-        for a in range(na):
+        for a in range(K_PASSES):
             for e in range(2):
-                nc.scalar.dma_start(tab_sw[4 * a + e : P : 16, :].bitcast(I32), tab_scales[a, e:16:2, :].bitcast(I32))
+                nc.scalar.dma_start(
+                    tab_bytes[LIVE * a + e : P : GROUP, :].bitcast(I32), tab_scales[a, e:BLOCKS:2, :].bitcast(I32)
+                )
+
         nc.sync.dma_start(list1[:], offs)
-        nc.sync.dma_start(wb_w_raw[:].bitcast(I32), wb_words[0].bitcast(I32))
+        nc.sync.dma_start(wb_loaded[:].bitcast(I32), wb_words[0].bitcast(I32))
         nc.sync.dma_start(list2[:], offs2)
-        load_words(tab2_w, tab2_words[0])
-        load_tab2_scales(0, 1, 2, 3)
+        for c0 in range(0, T, T // 2):
+            nc.sync.dma_start(
+                tab2_window[:, c0 : c0 + T // 2].bitcast(I32),
+                tab2_words[0, :, c0 : c0 + T // 2, :].rearrange("p t i -> p (t i)").bitcast(I32),
+            )
+        load_plane(tab2_bytes, tab2_scales[0], range(QUADS // 2))
         load_wf(0, 0)
-        load_words(tab_w[0], tab_words[0])
-        load_wb_scales(0, 1)
+        load_plane(tab2_bytes, tab2_scales[0], range(QUADS // 2, QUADS))
+        load_tab(0)
         load_wf(1, 0)
-        load_wb_scales(2, 3)
-        nc.sync.dma_start(gain_t[:], gain.rearrange("(b p t) -> p b t", b=nb, t=PACK))
-        load_words(tab_w[1], tab_words[1])
+        load_plane(wb_bytes, wb_scales[0], range(QUADS))
+        load_tab(1)
+        nc.sync.dma_start(gain_sb[:], gain.rearrange("(b p t) -> p b t", b=R_PASSES, t=PACK))
         load_wf(0, 1)
         load_seam(0, 0, pieces=2)
         load_wf(1, 1)
         load_seam(1, 0, pieces=2)
-        load_seam(0, 1)
-        load_seam(1, 1)
-        wq_w = held([P, nb, N], U32, "wq_w")
-        nc.sync.dma_start(wq_w[:].bitcast(I32), wq_words.rearrange("b p c i -> p b (c i)").bitcast(I32))
-        for q in range(4):
+        load_seam(0, 1, pieces=1)
+        load_seam(1, 1, pieces=1)
+        wq_sb = held([P, R_PASSES, N], U32, "wq_sb")
+        nc.sync.dma_start(wq_sb[:].bitcast(I32), wq_words.rearrange("b p c i -> p b (c i)").bitcast(I32))
+        for d in range(QUADS):
             nc.sync.dma_start(
-                wq_s[32 * q : 32 * q + 4, :, :].bitcast(I32),
-                wq_scales[:, 4 * q : 4 * q + 4, :].rearrange("b r n -> r b n").bitcast(I32),
+                wq_planes[QUAD * d : QUAD * d + LIVE, :, :].bitcast(I32),
+                wq_scales[:, LIVE * d : LIVE * (d + 1), :].rearrange("b q n -> q b n").bitcast(I32),
             )
         nc.sync.dma_start(list3[:], offs3)
-        wgo_t = held([P, S], F32, "wgo_t")
-        nc.sync.dma_start(wgo_t[:], wgo)
-        for i in range(ni):
-            load_page(i)
+        wgo_sb = held([P, S], F32, "wgo_sb")
+        nc.sync.dma_start(wgo_sb[:], wgo)
+        for nt in range(ROW_TILES):
+            page[nt] = held([P, T2], F32, "page%d" % nt)
+            nc.sync.dma_start(page[nt][:], page1[P * nt : P * (nt + 1), :])
 
-        v_sg = held([P, S], U8, "v_sg")
-        nc.vector.tensor_copy(v_sg[:], tab_sw[:].indirect(list1[:]))
-        v_s = held([P, S], U8, "v_s")
-        nc.vector.tensor_copy(v_s[:].bitcast(I32), v_sg[:].bitcast(I32))
-        for a in range(na):
+        v_bytes = held([P, S], U8, "v_bytes")
+        nc.vector.tensor_copy(v_bytes[:], tab_bytes[:].indirect(list1[:]))
+        v_planes = held([P, S], U8, "v_planes")
+        nc.vector.tensor_copy(v_planes[:].bitcast(I32), v_bytes[:].bitcast(I32))
+        for a in range(K_PASSES):
             for e in range(2):
                 nc.scalar.dma_start(
-                    v_s[4 * a + 2 + e : P : 32, :].bitcast(I32), v_sg[16 + 4 * a + e : P : 32, :].bitcast(I32)
+                    v_planes[LIVE * a + 2 + e : P : QUAD, :].bitcast(I32),
+                    v_bytes[GROUP + LIVE * a + e : P : QUAD, :].bitcast(I32),
                 )
-        v2_s = held([P, S], U8, "v2_s")
-        nc.vector.tensor_copy(v2_s[:], tab2_sw[:].indirect(list2[:]))
+        v2_plane = held([P, S], U8, "v2_plane")
+        nc.vector.tensor_copy(v2_plane[:], tab2_bytes[:].indirect(list2[:]))
 
-        wb_w = held([P, H], U16, "wb_w")
-        wb_s = held([P, H], U8, "wb_s")
-        nc.vector.tensor_copy(
-            wb_w[:].rearrange("p (b t m) -> p b m t", b=nb, t=PACK), wb_w_raw[:].rearrange("p (b m t) -> p b m t", b=nb, t=PACK)
-        )
+        def deal_wb(dealt, loaded):
+            nc.vector.tensor_copy(
+                dealt[:].rearrange("p (b t m) -> p b m t", b=R_PASSES, t=PACK),
+                loaded[:].rearrange("p (b m t) -> p b m t", b=R_PASSES, t=PACK),
+            )
 
-        v_w, v2_w, wf_w, wf_s, z_w, z_s = {}, {}, {}, {}, {}, {}
+        wb_sb = held([P, H], U16, "wb_sb")
+        wb_plane = held([P, H], U8, "wb_plane")
+        deal_wb(wb_sb, wb_loaded)
+
+        v_sb, v2_sb, wf_rounded, wf_sb, wf_plane = {}, {}, {}, {}, {}
 
         def gather_words(h):
-            cols = slice(LC * h, LC * (h + 1))
-            g = held([P, JC], U32, "v2_w%d" % h)
-            nc.vector.tensor_copy(g[:], tab2_w[:].indirect(list2[:, cols]))
-            v2_w[h] = g
-            for a in range(na):
-                g = held([P, JC], U32, "v_w%d%d" % (a, h))
-                nc.vector.tensor_copy(g[:], tab_w[a][:].indirect(list1[:, cols]))
-                v_w[a, h] = g
-
-        wf_grouped = {}
+            entries = slice(HALF // GROUP * h, HALF // GROUP * (h + 1))
+            v2_sb[h] = held([P, HALF], U32, "v2_sb%d" % h)
+            nc.vector.tensor_copy(v2_sb[h][:], tab2_window[:].indirect(list2[:, entries]))
+            for a in range(K_PASSES):
+                v_sb[a, h] = held([P, HALF], U32, "v_sb%d%d" % (a, h))
+                nc.vector.tensor_copy(v_sb[a, h][:], tab_window[a][:].indirect(list1[:, entries]))
 
         def round_wf(a, b):
-            wf_grouped[a, b] = stage.tile([P, KP * PACK], BF16, name="wf_grouped", align_bytes=64)
+            wf_rounded[a, b] = stage.tile([P, PASS * PACK], BF16, name="wf_rounded", align_bytes=64)
             nc.scalar.copy(
-                wf_grouped[a, b][:].rearrange("p (t m j) -> p m j t", t=PACK, j=PACK),
-                wf_raw[a, b][:].rearrange("p j (m t) -> p m j t", t=PACK),
+                wf_rounded[a, b][:].rearrange("p (t m i) -> p m i t", t=PACK, i=PACK),
+                wf_loaded[a, b][:].rearrange("p i (m t) -> p m i t", t=PACK),
             )
 
         def quantize_wf(a, b):
-            wf_w[a, b] = held([P, KP], U32, "wf_w%d%d" % (a, b))
-            wf_s[a, b] = held([P, KP], U8, "wf_s%d%d" % (a, b))
-            nc.vector.quantize_mx(out=wf_w[a, b][:].bitcast(FP8X4), scales=wf_s[a, b][:], in_=wf_grouped[a, b][:])
+            wf_sb[a, b] = held([P, PASS], U32, "wf_sb%d%d" % (a, b))
+            wf_plane[a, b] = held([P, PASS], U8, "wf_plane%d%d" % (a, b))
+            nc.vector.quantize_mx(out=wf_sb[a, b][:].bitcast(FP8X4), scales=wf_plane[a, b][:], in_=wf_rounded[a, b][:])
 
         def pattern(b, h, t):
-            u = seam_t[b, h]
-            mc = slice(KP * b + P * t, KP * b + P * (t + 1))
-            acc = psum.tile([P, JC], F32, name="pattern", bufs=3)
+            dealt_cols = slice(PASS * b + P * t, PASS * b + P * (t + 1))
+            acc = psum.tile([P, HALF], F32, name="pattern", bufs=3)
             nc.tensor.matmul_mx(
-                out=acc[:], lhsT=wb_w[:, mc].bitcast(FP4X4), lhsT_scale=wb_s[:, mc],
-                rhs=v2_w[h][:].bitcast(FP8X4), rhs_scale=v2_s[:, JC * h : JC * (h + 1)], start=True, stop=True,
+                out=acc[:], lhsT=wb_sb[:, dealt_cols].bitcast(FP4X4), lhsT_scale=wb_plane[:, dealt_cols],
+                rhs=v2_sb[h][:].bitcast(FP8X4), rhs_scale=v2_plane[:, HALF * h : HALF * (h + 1)], start=True, stop=True,
             )
-            nc.vector.tensor_tensor(u[:, t, :], acc[:], u[:, t, :], ALU.mult)
+            nc.vector.tensor_tensor(pre[b, h][:, t, :], acc[:], pre[b, h][:, t, :], ALU.mult)
 
         def fabric(b, h, t):
-            u = seam_t[b, h]
-            mc = slice(P * t, P * (t + 1))
-            acc = psum.tile([P, JC], F32, name="fabric", bufs=3)
-            for a in range(na):
+            slice_cols = slice(P * t, P * (t + 1))
+            acc = psum.tile([P, HALF], F32, name="fabric", bufs=3)
+            for a in range(K_PASSES):
                 nc.tensor.matmul_mx(
-                    out=acc[:], lhsT=wf_w[a, b][:, mc].bitcast(FP8X4), lhsT_scale=wf_s[a, b][:, mc],
-                    rhs=v_w[a, h][:].bitcast(FP8X4), rhs_scale=v_s[4 * a : P, JC * h : JC * (h + 1)],
-                    start=(a == 0), stop=(a == na - 1),
+                    out=acc[:],
+                    lhsT=wf_sb[a, b][:, slice_cols].bitcast(FP8X4), lhsT_scale=wf_plane[a, b][:, slice_cols],
+                    rhs=v_sb[a, h][:].bitcast(FP8X4), rhs_scale=v_planes[LIVE * a : P, HALF * h : HALF * (h + 1)],
+                    start=(a == 0), stop=(a == K_PASSES - 1),
                 )
-            nc.vector.tensor_tensor(u[:, t, :], acc[:], u[:, t, :], ALU.add)
+            nc.vector.tensor_tensor(pre[b, h][:, t, :], acc[:], pre[b, h][:, t, :], ALU.add)
 
-        def first_stage(b, h):
-            pattern(b, h, 0)
-            for t in range(PACK):
+        def first_stage(b, h, slices):
+            for t in slices:
+                if t == 0:
+                    pattern(b, h, 0)
                 if t + 1 < PACK:
                     pattern(b, h, t + 1)
                 fabric(b, h, t)
 
-        z_grouped, y = {}, {}
-        for h in range(nh):
-            for b in range(nb):
-                z_w[b, h] = held([P, JC], U32, "z_w%d%d" % (b, h))
-                z_s[b, h] = held([P, JC], U8, "z_s%d%d" % (b, h))
+        z_woven, z_sb, z_plane, y_sb = {}, {}, {}, {}
+        for h in range(S // HALF):
+            for b in range(R_PASSES):
+                z_sb[b, h] = held([P, HALF], U32, "z_sb%d%d" % (b, h))
+                z_plane[b, h] = held([P, HALF], U8, "z_plane%d%d" % (b, h))
 
-        def bend(b, j0, w, on_gpsimd=0, tag=None):
-            u, jc = seam_t[b, j0 // JC], slice(j0 % JC, j0 % JC + w)
-            if tag is None:
-                rows = stage.tile([P, PACK, w], BF16, name="z_rows", align_bytes=64)
+        def within_half(j0, width):
+            return j0 // HALF, slice(j0 % HALF, j0 % HALF + width)
+
+        def bend(b, j0, width, on_gpsimd=0, shared=None):
+            h, cols = within_half(j0, width)
+            if shared is None:
+                rows = stage.tile([P, PACK, width], BF16, name="z_rows", align_bytes=64)
             else:
-                rows = keep.tile([P, PACK, w], BF16, name="z_rows_" + tag, tag=tag, align_bytes=64)
+                rows = keep.tile([P, PACK, width], BF16, name="z_rows_" + shared, tag=shared, align_bytes=64)
             for t in range(PACK):
-                nc.scalar.activation(u[:, t, jc], u[:, t, jc], ACT.Tanh)
+                bent, factor = pre[b, h][:, t, cols], gain_sb[:, b, t : t + 1]
+                nc.scalar.activation(bent, bent, ACT.Tanh)
                 if t < on_gpsimd:
-                    nc.gpsimd.tensor_scalar(rows[:, t, :], u[:, t, jc], gain_t[:, b, t : t + 1], 0.0, ALU.mult, ALU.add)
+                    nc.gpsimd.tensor_scalar(rows[:, t, :], bent, factor, 0.0, ALU.mult, ALU.add)
                 else:
-                    nc.scalar.activation(rows[:, t, :], u[:, t, jc], ACT.Copy, scale=gain_t[:, b, t : t + 1])
+                    nc.scalar.activation(rows[:, t, :], bent, ACT.Copy, scale=factor)
             return rows
 
+        def woven_tile(b, j0, width):
+            z_woven[b, j0] = stage.tile([P, width * PACK], BF16, name="z_woven", bufs=3, align_bytes=64)
+            return z_woven[b, j0]
+
         def weave(b, j0, rows):
-            z_grouped[b, j0] = stage.tile([P, rows.shape[2] * PACK], BF16, name="z_grouped", bufs=3, align_bytes=64)
             nc.scalar.copy(
-                z_grouped[b, j0][:].rearrange("p (c i t) -> p c t i", i=4, t=PACK),
-                rows.rearrange("p t (c i) -> p c t i", i=4),
+                woven_tile(b, j0, rows.shape[2])[:].rearrange("p (c s t) -> p c t s", s=4, t=PACK),
+                rows.rearrange("p t (c s) -> p c t s", s=4),
             )
 
         def weave_on_gpsimd(b, j0, rows):
-            w = rows.shape[2]
-            z_grouped[b, j0] = stage.tile([P, w * PACK], BF16, name="z_grouped", bufs=3, align_bytes=64)
-            for c0 in range(0, w, w // 2):
+            width = rows.shape[2]
+            woven = woven_tile(b, j0, width)
+            for c0 in range(0, width, width // 2):
                 nc.gpsimd.tensor_scalar(
-                    z_grouped[b, j0][:, PACK * c0 : PACK * (c0 + w // 2)].rearrange("p (j t) -> p j t", t=PACK),
-                    rows[:, :, c0 : c0 + w // 2].rearrange("p t j -> p j t"), 1.0, 0.0, ALU.mult, ALU.add,
+                    woven[:, PACK * c0 : PACK * (c0 + width // 2)].rearrange("p (j t) -> p j t", t=PACK),
+                    rows[:, :, c0 : c0 + width // 2].rearrange("p t j -> p j t"), 1.0, 0.0, ALU.mult, ALU.add,
                 )
 
-        def quantize_z(b, j0, w):
-            h, jc = j0 // JC, slice(j0 % JC, j0 % JC + w)
-            nc.vector.quantize_mx(out=z_w[b, h][:, jc].bitcast(FP8X4), scales=z_s[b, h][:, jc], in_=z_grouped[b, j0][:])
-
-        def second_stage(i, j0, w, tag=None):
-            h, jc = j0 // JC, slice(j0 % JC, j0 % JC + w)
-            mc = slice(P * i, P * (i + 1))
-            if j0 < JC:
-                acc = psum.tile([P, w], F32, name="contrast", bufs=2)
-            else:
-                acc = psum.tile([P, w], F32, name="contrast_late", tag="pattern" if i % 2 == 0 else "fabric", bufs=3)
-            for b in range(nb):
-                nc.tensor.matmul_mx(
-                    out=acc[:], lhsT=wq_w[:, b, mc].bitcast(FP8X4), lhsT_scale=wq_s[:, b, mc],
-                    rhs=z_w[b, h][:, jc].bitcast(FP8X4), rhs_scale=z_s[b, h][:, jc],
-                    start=(b == 0), stop=(b == nb - 1),
-                )
-            if tag is None:
-                y[i, j0] = stage.tile([P, w], F32, name="y", bufs=4, align_bytes=64)
-            else:
-                y[i, j0] = keep.tile([P, w], F32, name="y_" + tag, tag=tag, align_bytes=64)
-            nc.scalar.copy(y[i, j0][:], acc[:])
-
-        def place(i, j0, w):
-            nc.vector.tensor_tensor(
-                page[i][:].indirect(list3[:, j0 // 16 : (j0 + w) // 16]), y[i, j0][:], wgo_t[:, j0 : j0 + w], ALU.mult
+        def quantize_z(b, j0, width):
+            h, cols = within_half(j0, width)
+            nc.vector.quantize_mx(
+                out=z_sb[b, h][:, cols].bitcast(FP8X4), scales=z_plane[b, h][:, cols], in_=z_woven[b, j0][:]
             )
-            if j0 + w == S:
-                nc.sync.dma_start(out[P * i : P * (i + 1), :], page[i][:])
 
-        Q3, Q4, QW = JC, JC + JC // 2, JC // 2
+        def second_stage(nt, j0, width, shared=None):
+            h, cols = within_half(j0, width)
+            rows_n = slice(P * nt, P * (nt + 1))
+            if h == 0:
+                acc = psum.tile([P, width], F32, name="contrast", bufs=2)
+            else:
+                acc = psum.tile([P, width], F32, name="contrast_late", tag=("pattern", "fabric")[nt % 2], bufs=3)
+            for b in range(R_PASSES):
+                nc.tensor.matmul_mx(
+                    out=acc[:], lhsT=wq_sb[:, b, rows_n].bitcast(FP8X4), lhsT_scale=wq_planes[:, b, rows_n],
+                    rhs=z_sb[b, h][:, cols].bitcast(FP8X4), rhs_scale=z_plane[b, h][:, cols],
+                    start=(b == 0), stop=(b == R_PASSES - 1),
+                )
+            if shared is None:
+                y_sb[nt, j0] = stage.tile([P, width], F32, name="y_sb", bufs=ROW_TILES, align_bytes=64)
+            else:
+                y_sb[nt, j0] = keep.tile([P, width], F32, name="y_sb_" + shared, tag=shared, align_bytes=64)
+            nc.scalar.copy(y_sb[nt, j0][:], acc[:])
+
+        def place(nt, j0, width):
+            nc.vector.tensor_tensor(
+                page[nt][:].indirect(list3[:, j0 // GROUP : (j0 + width) // GROUP]),
+                y_sb[nt, j0][:], wgo_sb[:, j0 : j0 + width], ALU.mult,
+            )
+            if j0 + width == S:
+                nc.sync.dma_start(out[P * nt : P * (nt + 1), :], page[nt][:])
+
         gather_words(0)
-        nc.vector.tensor_copy(
-            wb_s[:].rearrange("p (b t m) -> p b m t", b=nb, t=PACK), wb_s_raw[:].rearrange("p (b m t) -> p b m t", b=nb, t=PACK)
-        )
-        for a in range(na):
+        deal_wb(wb_plane, wb_bytes)
+        for a in range(K_PASSES):
             round_wf(a, 0)
             quantize_wf(a, 0)
         gather_words(1)
-        for a in range(na):
+        for a in range(K_PASSES):
             round_wf(a, 1)
-        first_stage(0, 0)
-        quantize_wf(0, 1)
-        pattern(1, 0, 0)
-        pattern(1, 0, 1)
-        quantize_wf(1, 1)
-        pattern(1, 0, 2)
-        pattern(1, 0, 3)
+
+        first_stage(0, 0, range(PACK))
+        for a in range(K_PASSES):
+            quantize_wf(a, 1)
+            pattern(1, 0, 2 * a)
+            pattern(1, 0, 2 * a + 1)
         for t in range(PACK):
             fabric(1, 0, t)
-        weave_on_gpsimd(0, 0, bend(0, 0, JC, on_gpsimd=3)[:])
-        weave(1, 0, bend(1, 0, JC, on_gpsimd=2)[:])
-        first_stage(0, 1)
-        quantize_z(0, 0, JC)
-        pattern(1, 1, 0)
-        pattern(1, 1, 1)
-        fabric(1, 1, 0)
-        quantize_z(1, 0, JC)
-        pattern(1, 1, 2)
-        fabric(1, 1, 1)
-        pattern(1, 1, 3)
-        fabric(1, 1, 2)
-        fabric(1, 1, 3)
-        for i in range(ni - 1):
-            second_stage(i, 0, JC)
-        low_rows = bend(0, JC, JC)
-        third_rows = bend(1, Q3, QW, tag="third")
-        weave(0, Q3, low_rows[:, :, :QW])
-        weave(1, Q3, third_rows[:])
-        for i in range(ni - 1):
-            place(i, 0, JC)
-        for b in range(nb):
-            quantize_z(b, Q3, QW)
-        second_stage(ni - 1, 0, JC, "third")
-        fourth_rows = bend(1, Q4, QW, tag="fourth")
-        weave(0, Q4, low_rows[:, :, QW:])
-        weave(1, Q4, fourth_rows[:])
-        place(ni - 1, 0, JC)
-        for b in range(nb):
-            quantize_z(b, Q4, QW)
-        second_stage(0, Q3, QW, "fourth")
-        second_stage(1, Q3, QW)
-        place(0, Q3, QW)
-        place(1, Q3, QW)
-        for i in (1, 0):
-            second_stage(i, Q4, QW)
-            place(i, Q4, QW)
-        for i in range(2, ni):
-            second_stage(i, JC, JC)
-            place(i, JC, JC)
+        weave_on_gpsimd(0, 0, bend(0, 0, HALF, on_gpsimd=GAINS_ON_GPSIMD[0])[:])
+        weave(1, 0, bend(1, 0, HALF, on_gpsimd=GAINS_ON_GPSIMD[1])[:])
+
+        first_stage(0, 1, range(PACK))
+        quantize_z(0, 0, HALF)
+        first_stage(1, 1, range(1))
+        quantize_z(1, 0, HALF)
+        first_stage(1, 1, range(1, PACK))
+
+        third, fourth, last = HALF, HALF + QUARTER, ROW_TILES - 1
+        for nt in range(last):
+            second_stage(nt, 0, HALF)
+        rows_pass0 = bend(0, HALF, HALF)
+        rows_third = bend(1, third, QUARTER, shared="third")
+        weave(0, third, rows_pass0[:, :, :QUARTER])
+        weave(1, third, rows_third[:])
+        for nt in range(last):
+            place(nt, 0, HALF)
+        for b in range(R_PASSES):
+            quantize_z(b, third, QUARTER)
+        second_stage(last, 0, HALF, shared="third")
+        rows_fourth = bend(1, fourth, QUARTER, shared="fourth")
+        weave(0, fourth, rows_pass0[:, :, QUARTER:])
+        weave(1, fourth, rows_fourth[:])
+        place(last, 0, HALF)
+        for b in range(R_PASSES):
+            quantize_z(b, fourth, QUARTER)
+
+        second_stage(0, third, QUARTER, shared="fourth")
+        second_stage(1, third, QUARTER)
+        place(0, third, QUARTER)
+        place(1, third, QUARTER)
+        for nt in (1, 0):
+            second_stage(nt, fourth, QUARTER)
+            place(nt, fourth, QUARTER)
+        for nt in range(2, ROW_TILES):
+            second_stage(nt, HALF, HALF)
+            place(nt, HALF, HALF)

from contextlib import ExitStack

import concourse.mybir as mybir

K, K2, H, N, T, S, T2 = 1024, 512, 1024, 512, 2048, 1024, 2048
FLOPS = 2 * S * (K * H + K2 * H + H * N)

F32 = mybir.dt.float32
BF16 = mybir.dt.bfloat16
I32 = mybir.dt.int32
U32 = mybir.dt.uint32
U16 = mybir.dt.uint16
U8 = mybir.dt.uint8
FP8X4 = mybir.dt.float8_e4m3fn_x4
FP4X4 = mybir.dt.float4_e2m1fn_x4
ACT = mybir.ActivationFunctionType
ALU = mybir.AluOpType

P = 128
PACK = 4
PASS = P * PACK
QUAD = 32
QUADS = P // QUAD
LIVE = 4
BLOCKS = QUADS * LIVE
GROUP = 16
HALF = 512
QUARTER = HALF // 2
K_PASSES, R_PASSES, ROW_TILES = K // PASS, H // PASS, N // P

GAINS_ON_GPSIMD = (3, 2)


def tile_list_quilt_patch_contrast_kernel(
    tc, tab_words, tab_scales, offs, tab2_words, tab2_scales, offs2, offs3, wf, wb_words, wb_scales,
    seam, gain, wq_words, wq_scales, wgo, page1, out,
):
    nc = tc.nc

    with ExitStack() as ctx:
        keep = ctx.enter_context(tc.tile_pool(name="keep", bufs=1))
        stage = ctx.enter_context(tc.tile_pool(name="stage", bufs=2))
        psum = ctx.enter_context(tc.psum_pool(name="psum", bufs=1))

        def held(shape, dtype, name):
            return keep.tile(shape, dtype, name=name, align_bytes=64)

        list1 = held([P, S // GROUP], U16, "list1")
        list2 = held([P, S // GROUP], U16, "list2")
        list3 = held([P, S // GROUP], U16, "list3")
        tab_bytes = held([P, T], U8, "tab_bytes")
        tab2_bytes = held([P, T], U8, "tab2_bytes")
        wb_bytes = held([P, H], U8, "wb_bytes")
        wq_planes = held([P, R_PASSES, N], U8, "wq_planes")
        nc.gpsimd.memset(tab_bytes[:].bitcast(I32), 0)
        nc.gpsimd.memset(wb_bytes[:].bitcast(I32), 0)
        nc.vector.memset(tab2_bytes[:].bitcast(I32), 0)
        nc.vector.memset(wq_planes[:].rearrange("p b n -> p (b n)").bitcast(I32), 0)

        tab2_window = held([P, T], U32, "tab2_window")
        tab_window = [held([P, T], U32, "tab_window%d" % a) for a in range(K_PASSES)]
        wb_loaded = held([P, H], U16, "wb_loaded")
        gain_sb = held([P, R_PASSES, PACK], F32, "gain_sb")
        wf_loaded, pre, page = {}, {}, {}

        def load_tab(a):
            nc.sync.dma_start(tab_window[a][:].bitcast(I32), tab_words[a].rearrange("p t i -> p (t i)").bitcast(I32))

        def load_plane(tile, scales, quads):
            for d in quads:
                nc.sync.dma_start(
                    tile[QUAD * d : QUAD * d + LIVE, :].bitcast(I32), scales[LIVE * d : LIVE * (d + 1), :].bitcast(I32)
                )

        def load_wf(a, b):
            wf_loaded[a, b] = held([P, PACK, PASS], F32, "wf_loaded%d%d" % (a, b))
            nc.sync.dma_start(
                wf_loaded[a, b][:],
                wf[PASS * a : PASS * (a + 1), PASS * b : PASS * (b + 1)].rearrange("(p i) c -> p i c", i=PACK),
            )

        def load_seam(b, h, pieces):
            pre[b, h] = held([P, PACK, HALF], F32, "pre%d%d" % (b, h))
            source = seam[PASS * b : PASS * (b + 1), HALF * h : HALF * (h + 1)].rearrange("(p t) j -> p t j", t=PACK)
            for t0 in range(0, PACK, PACK // pieces):
                nc.sync.dma_start(pre[b, h][:, t0 : t0 + PACK // pieces, :], source[:, t0 : t0 + PACK // pieces, :])

        for a in range(K_PASSES):
            for e in range(2):
                nc.scalar.dma_start(
                    tab_bytes[LIVE * a + e : P : GROUP, :].bitcast(I32), tab_scales[a, e:BLOCKS:2, :].bitcast(I32)
                )

        nc.sync.dma_start(list1[:], offs)
        nc.sync.dma_start(wb_loaded[:].bitcast(I32), wb_words[0].bitcast(I32))
        nc.sync.dma_start(list2[:], offs2)
        for c0 in range(0, T, T // 2):
            nc.sync.dma_start(
                tab2_window[:, c0 : c0 + T // 2].bitcast(I32),
                tab2_words[0, :, c0 : c0 + T // 2, :].rearrange("p t i -> p (t i)").bitcast(I32),
            )
        load_plane(tab2_bytes, tab2_scales[0], range(QUADS // 2))
        load_wf(0, 0)
        load_plane(tab2_bytes, tab2_scales[0], range(QUADS // 2, QUADS))
        load_tab(0)
        load_wf(1, 0)
        load_plane(wb_bytes, wb_scales[0], range(QUADS))
        load_tab(1)
        nc.sync.dma_start(gain_sb[:], gain.rearrange("(b p t) -> p b t", b=R_PASSES, t=PACK))
        load_wf(0, 1)
        load_seam(0, 0, pieces=2)
        load_wf(1, 1)
        load_seam(1, 0, pieces=2)
        load_seam(0, 1, pieces=1)
        load_seam(1, 1, pieces=1)
        wq_sb = held([P, R_PASSES, N], U32, "wq_sb")
        nc.sync.dma_start(wq_sb[:].bitcast(I32), wq_words.rearrange("b p c i -> p b (c i)").bitcast(I32))
        for d in range(QUADS):
            nc.sync.dma_start(
                wq_planes[QUAD * d : QUAD * d + LIVE, :, :].bitcast(I32),
                wq_scales[:, LIVE * d : LIVE * (d + 1), :].rearrange("b q n -> q b n").bitcast(I32),
            )
        nc.sync.dma_start(list3[:], offs3)
        wgo_sb = held([P, S], F32, "wgo_sb")
        nc.sync.dma_start(wgo_sb[:], wgo)
        for nt in range(ROW_TILES):
            page[nt] = held([P, T2], F32, "page%d" % nt)
            nc.sync.dma_start(page[nt][:], page1[P * nt : P * (nt + 1), :])

        v_bytes = held([P, S], U8, "v_bytes")
        nc.vector.tensor_copy(v_bytes[:], tab_bytes[:].indirect(list1[:]))
        v_planes = held([P, S], U8, "v_planes")
        nc.vector.tensor_copy(v_planes[:].bitcast(I32), v_bytes[:].bitcast(I32))
        for a in range(K_PASSES):
            for e in range(2):
                nc.scalar.dma_start(
                    v_planes[LIVE * a + 2 + e : P : QUAD, :].bitcast(I32),
                    v_bytes[GROUP + LIVE * a + e : P : QUAD, :].bitcast(I32),
                )
        v2_plane = held([P, S], U8, "v2_plane")
        nc.vector.tensor_copy(v2_plane[:], tab2_bytes[:].indirect(list2[:]))

        def deal_wb(dealt, loaded):
            nc.vector.tensor_copy(
                dealt[:].rearrange("p (b t m) -> p b m t", b=R_PASSES, t=PACK),
                loaded[:].rearrange("p (b m t) -> p b m t", b=R_PASSES, t=PACK),
            )

        wb_sb = held([P, H], U16, "wb_sb")
        wb_plane = held([P, H], U8, "wb_plane")
        deal_wb(wb_sb, wb_loaded)

        v_sb, v2_sb, wf_rounded, wf_sb, wf_plane = {}, {}, {}, {}, {}

        def gather_words(h):
            entries = slice(HALF // GROUP * h, HALF // GROUP * (h + 1))
            v2_sb[h] = held([P, HALF], U32, "v2_sb%d" % h)
            nc.vector.tensor_copy(v2_sb[h][:], tab2_window[:].indirect(list2[:, entries]))
            for a in range(K_PASSES):
                v_sb[a, h] = held([P, HALF], U32, "v_sb%d%d" % (a, h))
                nc.vector.tensor_copy(v_sb[a, h][:], tab_window[a][:].indirect(list1[:, entries]))

        def round_wf(a, b):
            wf_rounded[a, b] = stage.tile([P, PASS * PACK], BF16, name="wf_rounded", align_bytes=64)
            nc.scalar.copy(
                wf_rounded[a, b][:].rearrange("p (t m i) -> p m i t", t=PACK, i=PACK),
                wf_loaded[a, b][:].rearrange("p i (m t) -> p m i t", t=PACK),
            )

        def quantize_wf(a, b):
            wf_sb[a, b] = held([P, PASS], U32, "wf_sb%d%d" % (a, b))
            wf_plane[a, b] = held([P, PASS], U8, "wf_plane%d%d" % (a, b))
            nc.vector.quantize_mx(out=wf_sb[a, b][:].bitcast(FP8X4), scales=wf_plane[a, b][:], in_=wf_rounded[a, b][:])

        def pattern(b, h, t):
            dealt_cols = slice(PASS * b + P * t, PASS * b + P * (t + 1))
            acc = psum.tile([P, HALF], F32, name="pattern", bufs=3)
            nc.tensor.matmul_mx(
                out=acc[:], lhsT=wb_sb[:, dealt_cols].bitcast(FP4X4), lhsT_scale=wb_plane[:, dealt_cols],
                rhs=v2_sb[h][:].bitcast(FP8X4), rhs_scale=v2_plane[:, HALF * h : HALF * (h + 1)], start=True, stop=True,
            )
            nc.vector.tensor_tensor(pre[b, h][:, t, :], acc[:], pre[b, h][:, t, :], ALU.mult)

        def fabric(b, h, t):
            slice_cols = slice(P * t, P * (t + 1))
            acc = psum.tile([P, HALF], F32, name="fabric", bufs=3)
            for a in range(K_PASSES):
                nc.tensor.matmul_mx(
                    out=acc[:],
                    lhsT=wf_sb[a, b][:, slice_cols].bitcast(FP8X4), lhsT_scale=wf_plane[a, b][:, slice_cols],
                    rhs=v_sb[a, h][:].bitcast(FP8X4), rhs_scale=v_planes[LIVE * a : P, HALF * h : HALF * (h + 1)],
                    start=(a == 0), stop=(a == K_PASSES - 1),
                )
            nc.vector.tensor_tensor(pre[b, h][:, t, :], acc[:], pre[b, h][:, t, :], ALU.add)

        def first_stage(b, h, slices):
            for t in slices:
                if t == 0:
                    pattern(b, h, 0)
                if t + 1 < PACK:
                    pattern(b, h, t + 1)
                fabric(b, h, t)

        z_woven, z_sb, z_plane, y_sb = {}, {}, {}, {}
        for h in range(S // HALF):
            for b in range(R_PASSES):
                z_sb[b, h] = held([P, HALF], U32, "z_sb%d%d" % (b, h))
                z_plane[b, h] = held([P, HALF], U8, "z_plane%d%d" % (b, h))

        def within_half(j0, width):
            return j0 // HALF, slice(j0 % HALF, j0 % HALF + width)

        def bend(b, j0, width, on_gpsimd=0, shared=None):
            h, cols = within_half(j0, width)
            if shared is None:
                rows = stage.tile([P, PACK, width], BF16, name="z_rows", align_bytes=64)
            else:
                rows = keep.tile([P, PACK, width], BF16, name="z_rows_" + shared, tag=shared, align_bytes=64)
            for t in range(PACK):
                bent, factor = pre[b, h][:, t, cols], gain_sb[:, b, t : t + 1]
                nc.scalar.activation(bent, bent, ACT.Tanh)
                if t < on_gpsimd:
                    nc.gpsimd.tensor_scalar(rows[:, t, :], bent, factor, 0.0, ALU.mult, ALU.add)
                else:
                    nc.scalar.activation(rows[:, t, :], bent, ACT.Copy, scale=factor)
            return rows

        def woven_tile(b, j0, width):
            z_woven[b, j0] = stage.tile([P, width * PACK], BF16, name="z_woven", bufs=3, align_bytes=64)
            return z_woven[b, j0]

        def weave(b, j0, rows):
            nc.scalar.copy(
                woven_tile(b, j0, rows.shape[2])[:].rearrange("p (c s t) -> p c t s", s=4, t=PACK),
                rows.rearrange("p t (c s) -> p c t s", s=4),
            )

        def weave_on_gpsimd(b, j0, rows):
            width = rows.shape[2]
            woven = woven_tile(b, j0, width)
            for c0 in range(0, width, width // 2):
                nc.gpsimd.tensor_scalar(
                    woven[:, PACK * c0 : PACK * (c0 + width // 2)].rearrange("p (j t) -> p j t", t=PACK),
                    rows[:, :, c0 : c0 + width // 2].rearrange("p t j -> p j t"), 1.0, 0.0, ALU.mult, ALU.add,
                )

        def quantize_z(b, j0, width):
            h, cols = within_half(j0, width)
            nc.vector.quantize_mx(
                out=z_sb[b, h][:, cols].bitcast(FP8X4), scales=z_plane[b, h][:, cols], in_=z_woven[b, j0][:]
            )

        def second_stage(nt, j0, width, shared=None):
            h, cols = within_half(j0, width)
            rows_n = slice(P * nt, P * (nt + 1))
            if h == 0:
                acc = psum.tile([P, width], F32, name="contrast", bufs=2)
            else:
                acc = psum.tile([P, width], F32, name="contrast_late", tag=("pattern", "fabric")[nt % 2], bufs=3)
            for b in range(R_PASSES):
                nc.tensor.matmul_mx(
                    out=acc[:], lhsT=wq_sb[:, b, rows_n].bitcast(FP8X4), lhsT_scale=wq_planes[:, b, rows_n],
                    rhs=z_sb[b, h][:, cols].bitcast(FP8X4), rhs_scale=z_plane[b, h][:, cols],
                    start=(b == 0), stop=(b == R_PASSES - 1),
                )
            if shared is None:
                y_sb[nt, j0] = stage.tile([P, width], F32, name="y_sb", bufs=ROW_TILES, align_bytes=64)
            else:
                y_sb[nt, j0] = keep.tile([P, width], F32, name="y_sb_" + shared, tag=shared, align_bytes=64)
            nc.scalar.copy(y_sb[nt, j0][:], acc[:])

        def place(nt, j0, width):
            nc.vector.tensor_tensor(
                page[nt][:].indirect(list3[:, j0 // GROUP : (j0 + width) // GROUP]),
                y_sb[nt, j0][:], wgo_sb[:, j0 : j0 + width], ALU.mult,
            )
            if j0 + width == S:
                nc.sync.dma_start(out[P * nt : P * (nt + 1), :], page[nt][:])

        gather_words(0)
        deal_wb(wb_plane, wb_bytes)
        for a in range(K_PASSES):
            round_wf(a, 0)
            quantize_wf(a, 0)
        gather_words(1)
        for a in range(K_PASSES):
            round_wf(a, 1)

        first_stage(0, 0, range(PACK))
        for a in range(K_PASSES):
            quantize_wf(a, 1)
            pattern(1, 0, 2 * a)
            pattern(1, 0, 2 * a + 1)
        for t in range(PACK):
            fabric(1, 0, t)
        weave_on_gpsimd(0, 0, bend(0, 0, HALF, on_gpsimd=GAINS_ON_GPSIMD[0])[:])
        weave(1, 0, bend(1, 0, HALF, on_gpsimd=GAINS_ON_GPSIMD[1])[:])

        first_stage(0, 1, range(PACK))
        quantize_z(0, 0, HALF)
        first_stage(1, 1, range(1))
        quantize_z(1, 0, HALF)
        first_stage(1, 1, range(1, PACK))

        third, fourth, last = HALF, HALF + QUARTER, ROW_TILES - 1
        for nt in range(last):
            second_stage(nt, 0, HALF)
        rows_pass0 = bend(0, HALF, HALF)
        rows_third = bend(1, third, QUARTER, shared="third")
        weave(0, third, rows_pass0[:, :, :QUARTER])
        weave(1, third, rows_third[:])
        for nt in range(last):
            place(nt, 0, HALF)
        for b in range(R_PASSES):
            quantize_z(b, third, QUARTER)
        second_stage(last, 0, HALF, shared="third")
        rows_fourth = bend(1, fourth, QUARTER, shared="fourth")
        weave(0, fourth, rows_pass0[:, :, QUARTER:])
        weave(1, fourth, rows_fourth[:])
        place(last, 0, HALF)
        for b in range(R_PASSES):
            quantize_z(b, fourth, QUARTER)

        second_stage(0, third, QUARTER, shared="fourth")
        second_stage(1, third, QUARTER)
        place(0, third, QUARTER)
        place(1, third, QUARTER)
        for nt in (1, 0):
            second_stage(nt, fourth, QUARTER)
            place(nt, fourth, QUARTER)
        for nt in range(2, ROW_TILES):
            second_stage(nt, HALF, HALF)
            place(nt, HALF, HALF)
